import numpy as np
import ml_dtypes


def mxq(x, axis, fmt="e4m3"):
    dtype, down = {"e4m3": (ml_dtypes.float8_e4m3fn, 7), "e5m2": (ml_dtypes.float8_e5m2, 14)}[fmt]
    v = np.moveaxis(np.asarray(x, np.float32).astype(ml_dtypes.bfloat16).astype(np.float64), axis, -1)
    blocks = v.reshape(v.shape[:-1] + (-1, 32))
    amax = np.abs(blocks).max(-1, keepdims=True)
    byte = np.maximum(np.where(amax > 0, np.frexp(amax)[1] - 1 + 127, 0) - down, 1)
    scale = np.exp2(byte - 127.0)
    codes = (blocks / scale).astype(np.float32).astype(dtype).astype(np.float64)
    return np.moveaxis((codes * scale).reshape(v.shape), -1, axis)


WIDE = False


def mx_kscale(k):
    if not WIDE:
        return np.ones(k)
    levels = np.array([10, -10, 5, -5, 0])
    if k % 512:
        return np.exp2(np.random.permutation(np.resize(levels, k // 32))).repeat(32)
    a = np.empty((k // 512, 16))
    for p in range(k // 512):
        a[p, :8] = np.random.permutation(np.resize(levels, 8))
        for g in range(8):
            far = levels[np.abs(levels - a[p, g]) >= 10]
            a[p, g + 8] = far[np.random.randint(len(far))]
    return np.exp2(a.ravel()).repeat(32)


BF16 = ml_dtypes.bfloat16


def bf(x):
    return np.asarray(x, np.float32).astype(BF16)


def f64(x):
    return np.asarray(x).astype(np.float64)


E2M1 = np.array([0.0, 0.5, 1.0, 1.5, 2.0, 3.0, 4.0, 6.0, -0.0, -0.5, -1.0, -1.5, -2.0, -3.0, -4.0, -6.0])


def pack_weight(w, fmt):
    k, n = w.shape
    w = f64(bf(w)).reshape(k // 32, 32, n)
    amax = np.abs(w).max(1)
    if fmt == "e4m3":
        byte = np.frexp(amax)[1] - 1 + 127 - 7
    else:
        mant, ex = np.frexp(amax / 6.0)
        byte = np.where(mant > 0.5, ex, ex - 1) + 127
    byte = np.clip(np.where(amax > 0, byte, 1), 1, 254)
    scaled = (w * np.exp2(127.0 - byte)[:, None, :]).reshape(k, n).astype(np.float32)
    by_word = np.ascontiguousarray(scaled.reshape(k // 512, 128, 4, n).transpose(0, 1, 3, 2))
    if fmt == "e4m3":
        words = by_word.astype(ml_dtypes.float8_e4m3fn).view(np.uint8)
    else:
        c = by_word.astype(ml_dtypes.float4_e2m1fn).view(np.uint8) & 0xF
        words = c[..., 0::2] | (c[..., 1::2] << 4)
    return np.ascontiguousarray(words), np.ascontiguousarray(byte.astype(np.uint8).reshape(k // 512, 16, n))


def unpack_weight(words, scales, fmt):
    g, p, n, _ = words.shape
    if fmt == "e4m3":
        vals = np.ascontiguousarray(words).view(ml_dtypes.float8_e4m3fn).astype(np.float64)
    else:
        nib = np.empty((g, p, n, 4), np.uint8)
        nib[..., 0::2] = words & 0xF
        nib[..., 1::2] = words >> 4
        vals = E2M1[nib]
    vals = vals * np.repeat(np.exp2(scales.astype(np.float64) - 127.0), 8, axis=1)[..., None]
    return vals.transpose(0, 1, 3, 2).reshape(g * 512, n)
def pack4(w):
    words, scales = pack_weight(w, "e2m1")
    return words.reshape(words.shape[0], 128, -1), scales


def unpack4(words, scales):
    return unpack_weight(words.reshape(words.shape[0], 128, -1, 2), scales, "e2m1")


T, E, H, D, S = 256, 1024, 16, 512, 1024

THETA = 10000.0


def sigmoid(v):
    return 1.0 / (1.0 + np.exp(-v))


def rotate_pairs(v, c, s):
    even, odd = v[:, :, 0::2], v[:, :, 1::2]
    c, s = c[:, None, :], s[:, None, :]
    return np.stack([even * c - odd * s, even * s + odd * c], axis=-1).reshape(v.shape)


def draw0():
    s = mx_kscale(E)
    t = mx_kscale(D)
    wq_words, wq_scales = pack4(np.random.standard_normal((E, H * D)) / np.sqrt(E) / s[:, None])
    k_words, k_scales = pack_weight(np.random.standard_normal((D, S)) / t[:, None], "e4m3")
    position = np.random.uniform(S, S + S, (T, 1))
    angle = position * THETA ** (-np.arange(D // 2) / (D // 2))
    return {"x": bf(np.random.standard_normal((T, E)) * s),
            "wq_words": wq_words,
            "wq_scales": wq_scales,
            "bias": bf(0.4 * np.random.standard_normal(H * D)),
            "gain": bf((1.0 + 0.1 * np.random.standard_normal((H, D))) * t),
            "cosines": bf(np.cos(angle)),
            "sines": bf(np.sin(angle)),
            "k_words": k_words,
            "k_scales": k_scales,
            "key_bias": bf(0.4 * np.random.standard_normal(S)),
            "head_gate": bf(np.random.standard_normal((T, H)))}


def core(x, wq_words, wq_scales, bias, gain, cosines, sines, k_words, k_scales, key_bias, head_gate):
    wq = unpack4(wq_words, wq_scales)
    keys = unpack_weight(k_words, k_scales, "e4m3")
    y = (mxq(f64(x), 1, "e4m3") @ wq) + f64(bias)
    y = y.reshape(T, H, D)
    y = y / np.sqrt(np.mean(y * y, axis=2, keepdims=True)) * f64(gain)
    z = rotate_pairs(y, f64(cosines), f64(sines))
    u = (mxq(z.reshape(T * H, D), 1, "e4m3") @ keys) / np.sqrt(D)
    u = np.maximum(u + f64(key_bias), 0.0).reshape(T, H, S)
    alpha = sigmoid(f64(head_gate))
    return np.sum(alpha[:, :, None] * u, axis=1) / np.sqrt(H)


def e4m3fn_bytes(y):
    return np.clip(np.asarray(y, np.float64), -448.0, 448.0).astype(np.float32).astype(ml_dtypes.float8_e4m3fn).view(np.uint8)


def e4m3fn_values(b):
    return np.asarray(b, np.uint8).view(ml_dtypes.float8_e4m3fn).astype(np.float64)


def setup_inputs():
    d = draw0()
    x0 = np.asarray(d['x']).astype(np.float64)
    s = (np.max(np.abs(x0), axis=(0,), keepdims=True) / 448.0).astype(np.float32)
    out = {}
    for k, v in d.items():
        if k == 'x':
            out['x_bytes'] = e4m3fn_bytes(x0 / s.astype(np.float64))
            out['x_scale'] = s
        else:
            out[k] = v
    return out


def reference(x_bytes, x_scale, wq_words, wq_scales, bias, gain, cosines, sines, k_words, k_scales, key_bias, head_gate):
    return core(e4m3fn_values(x_bytes) * x_scale.astype(np.float64), wq_words, wq_scales, bias, gain, cosines, sines, k_words, k_scales, key_bias, head_gate)

@@ -1,0 +1,314 @@
+import math
+from contextlib import ExitStack
+
+import concourse.mybir as mybir
+from concourse.masks import make_identity
+
+T, E, H, D, S = 256, 1024, 16, 512, 1024
+FLOPS = 2 * T * E * H * D + 2 * T * H * D * S
+
+F32 = mybir.dt.float32
+BF16 = mybir.dt.bfloat16
+I32 = mybir.dt.int32
+U32 = mybir.dt.uint32
+U8 = mybir.dt.uint8
+FP8 = mybir.dt.float8_e4m3fn
+FP8X4 = mybir.dt.float8_e4m3fn_x4
+FP4X4 = mybir.dt.float4_e2m1fn_x4
+ALU = mybir.AluOpType
+ACT = mybir.ActivationFunctionType
+
+P = 128
+G = E // 512
+NA = T // P
+NQ = 4
+ROOT_D = math.sqrt(D)
+MX2_LAG = 7
+
+
+def tile_shared_key_index_scores_f7_kernel(
+    tc, x_bytes, x_scale, wq_words, wq_scales, bias, gain, cosines, sines,
+    k_words, k_scales, key_bias, head_gate, out,
+):
+    nc = tc.nc
+    with ExitStack() as ctx:
+        keep = ctx.enter_context(tc.tile_pool(name="keep", bufs=1))
+        work = ctx.enter_context(tc.tile_pool(name="work", bufs=3))
+        psum = ctx.enter_context(tc.psum_pool(name="psum", bufs=1))
+        ctx.enter_context(tc.manual_schedule())
+
+        hg = keep.tile([P, NA, H], BF16, name="hg")
+        nc.scalar.dma_start(out=hg[:], in_=head_gate.rearrange("(a p) h -> p a h", p=P))
+        gb_rows = keep.tile([P, P], BF16, name="gb_rows")
+        nc.scalar.dma_start(out=gb_rows[0:64, :], in_=gain.rearrange("h (c m) -> (h c) m", m=P))
+        nc.scalar.dma_start(out=gb_rows[64:128, :], in_=bias.rearrange("(c m) -> c m", m=P))
+
+        xb = keep.tile([P, NA, E], U8, name="xb", align_bytes=64)
+        nc.sync.dma_start(out=xb[:], in_=x_bytes.rearrange("(a p) k -> p a k", p=P))
+        xs = keep.tile([P, E], F32, name="xs")
+        nc.sync.dma_start(out=xs[:], in_=x_scale.rearrange("o k -> (o k)").partition_broadcast(P))
+
+        wsc0 = keep.tile([P, G, 2048], U8, name="wsc0", align_bytes=64)
+        wscr = keep.tile([P, G, 6144], U8, name="wscr", align_bytes=64)
+        ksc = keep.tile([P, S], U8, name="ksc", align_bytes=64)
+        kb_rows = keep.tile([P, P], BF16, name="kb_rows")
+        nc.vector.memset(wsc0[:].rearrange("p g n -> p (g n)").bitcast(I32), 0)
+        nc.vector.memset(kb_rows[:], 0.0)
+        nc.vector.memset(wscr[:].rearrange("p g n -> p (g n)").bitcast(I32), 0)
+        nc.vector.memset(ksc[:].bitcast(I32), 0)
+
+        nc.scalar.dma_start(out=kb_rows[0:8, :], in_=key_bias.rearrange("(c m) -> c m", m=P))
+        for q in range(4):
+            nc.sync.dma_start(
+                out=wsc0[32 * q : 32 * q + 4, :, :].bitcast(I32),
+                in_=wq_scales[:, 4 * q : 4 * q + 4, 0:2048].rearrange("g r n -> r g n").bitcast(I32),
+            )
+        wt = []
+        for b in range(NQ):
+            w = keep.tile([P, G, 4096], U8, name=f"w{b}", align_bytes=64)
+            wt.append(w)
+        nc.sync.dma_start(out=wt[0][:], in_=wq_words[:, :, 0:4096].rearrange("g p n -> p g n"))
+        cs = keep.tile([P, NA, D // 2], BF16, name="cs")
+        sn = keep.tile([P, NA, D // 2], BF16, name="sn")
+        nc.sync.dma_start(out=cs[:], in_=cosines.rearrange("(a p) r -> p a r", p=P))
+        nc.sync.dma_start(out=sn[:], in_=sines.rearrange("(a p) r -> p a r", p=P))
+        for q in range(4):
+            nc.sync.dma_start(
+                out=wscr[32 * q : 32 * q + 4, :, :].bitcast(I32),
+                in_=wq_scales[:, 4 * q : 4 * q + 4, 2048:8192].rearrange("g r n -> r g n").bitcast(I32),
+            )
+        nc.sync.dma_start(out=wt[1][:], in_=wq_words[:, :, 4096:8192].rearrange("g p n -> p g n"))
+        for q in range(4):
+            nc.sync.dma_start(
+                out=ksc[32 * q : 32 * q + 4, :].bitcast(I32),
+                in_=k_scales[0, 4 * q : 4 * q + 4, :].bitcast(I32),
+            )
+        kc = keep.tile([P, 4 * S], U8, name="kc", align_bytes=64)
+        nc.sync.dma_start(out=kc[:], in_=k_words[0].rearrange("p n t -> p (n t)"))
+        kb_all = keep.tile([P, S], BF16, name="kb_all")
+        nc.sync.dma_start(out=kb_all[:], in_=key_bias.partition_broadcast(P))
+        for b in range(2, NQ):
+            nc.sync.dma_start(
+                out=wt[b][:], in_=wq_words[:, :, 4096 * b : 4096 * (b + 1)].rearrange("g p n -> p g n")
+            )
+
+        ident = keep.tile([P, P], F32, name="ident")
+        make_identity(nc, ident[:])
+        identb = keep.tile([P, P], BF16, name="identb")
+        make_identity(nc, identb[:])
+
+        alpha = keep.tile([P, NA, H], F32, name="alpha")
+        asum = keep.tile([P, NA], F32, name="asum")
+        for a in range(NA):
+            nc.scalar.activation(out=alpha[:, a, :], in_=hg[:, a, :], func=ACT.Sigmoid, accum_out=asum[:, a : a + 1])
+        alpha_s = keep.tile([P, NA, H], F32, name="alpha_s")
+        nc.vector.tensor_scalar(out=alpha_s[:], in0=alpha[:], scalar1=1.0 / (4.0 * ROOT_D), scalar2=None, op0=ALU.mult)
+        asum4 = keep.tile([P, NA], F32, name="asum4")
+        nc.vector.tensor_scalar(out=asum4[:], in0=asum[:], scalar1=0.25, scalar2=None, op0=ALU.mult)
+        warm = keep.tile([P, 1], F32, name="warm")
+        nc.scalar.activation(out=warm[:], in_=asum[:, 0:1], func=ACT.Sqrt)
+
+        cols_ps = psum.tile([P, 2, P], BF16, name="cols_ps", tag="u", bufs=2)
+        nc.tensor.transpose(cols_ps[:, 0, :], gb_rows[:], identb[:])
+        nc.tensor.transpose(cols_ps[:, 1, :], kb_rows[:], identb[:])
+        gcol = keep.tile([P, 64], F32, name="gcol")
+        bcol = keep.tile([P, 64], F32, name="bcol")
+        gbcol = keep.tile([P, 64], F32, name="gbcol")
+        nkb = keep.tile([P, 8], F32, name="nkb")
+        nc.vector.tensor_copy(out=gcol[:], in_=cols_ps[:, 0, 0:64])
+        nc.vector.tensor_copy(out=bcol[:], in_=cols_ps[:, 0, 64:128])
+        nc.vector.tensor_scalar(out=nkb[:], in0=cols_ps[:, 1, 0:8], scalar1=-ROOT_D, scalar2=None, op0=ALU.mult)
+        nc.vector.tensor_tensor(out=gbcol[:], in0=gcol[:], in1=bcol[:], op=ALU.mult)
+
+        alpha_t = keep.tile([P, NA, H, P], F32, name="alpha_t")
+        for a in range(NA):
+            for b in range(NQ):
+                at_ps = psum.tile([P, 4, P], F32, name="at_ps", tag="u", bufs=2)
+                for hh in range(4):
+                    h = 4 * b + hh
+                    nc.tensor.transpose(at_ps[:, hh, :], alpha_s[:, a, h : h + 1].to_broadcast([P, P]), ident[:])
+                nc.scalar.copy(out=alpha_t[:, a, 4 * b : 4 * b + 4, :], in_=at_ps[:])
+
+        cos_d = keep.tile([P, NA, D // 2, 2], BF16, name="cos_d")
+        sin_s = keep.tile([P, NA, D // 2, 2], BF16, name="sin_s")
+        for a in range(NA):
+            for e in range(2):
+                nc.gpsimd.tensor_scalar(out=cos_d[:, a, :, e], in0=cs[:, a, :], scalar1=1.0, scalar2=0.0, op0=ALU.mult, op1=ALU.add)
+                sign = 1.0 if e else -1.0
+                nc.gpsimd.tensor_scalar(out=sin_s[:, a, :, e], in0=sn[:, a, :], scalar1=sign, scalar2=0.0, op0=ALU.mult, op1=ALU.add)
+
+        xp = keep.tile([P, NA, E], BF16, name="xp", align_bytes=64)
+        for a in range(NA):
+            nc.vector.tensor_tensor(out=xp[:, a, :], in0=xb[:, a, :].bitcast(FP8), in1=xs[:], op=ALU.mult)
+        xc = keep.tile([P, G, T], U32, name="xc", align_bytes=64)
+        xcs = keep.tile([P, G, T], U8, name="xcs", align_bytes=64)
+        xg = keep.tile([P, G, T * 4], BF16, name="xg", align_bytes=64)
+        for g in range(G):
+            xt_ps = psum.tile([P, NA, 2, P], F32, name="xt_ps", tag="t1", bufs=2)
+            for a in range(NA):
+                words = xp[:, a, :].bitcast(F32)
+                for u in range(2):
+                    nc.tensor.transpose(xt_ps[:, a, u, :], words[:, 256 * g + u : 256 * (g + 1) : 2], ident[:])
+            nc.vector.tensor_copy(
+                out=xg[:, g, :].bitcast(F32).rearrange("p (a i u) -> p a i u", a=NA, u=2),
+                in_=xt_ps[:].rearrange("p a u i -> p a i u"),
+            )
+        for g in range(G):
+            nc.vector.quantize_mx(out=xc[:, g, :].bitcast(FP8X4), scales=xcs[:, g, :], in_=xg[:, g, :])
+
+        units = NA * H
+        yg_of, sq_of, t1_of, rinv_of, pq_of, z_of = {}, {}, {}, {}, {}, {}
+        grp_of, zc_of, zs_of, v_of = {}, {}, {}, {}
+        acc = {}
+        misc = None
+        for n in range(units + MX2_LAG + 2):
+            if n < units:
+                a, h = divmod(n, H)
+                b, hq = divmod(h, 4)
+                mx1 = psum.tile([P, 4, P], F32, name="mx1", tag="mx1", bufs=1)
+                for c in range(4):
+                    for g in range(G):
+                        if b == 0:
+                            scale = wsc0[:, g, 512 * hq + P * c : 512 * hq + P * (c + 1)]
+                        else:
+                            col = 512 * (h - 4) + P * c
+                            scale = wscr[:, g, col : col + P]
+                        byte = 1024 * hq + 256 * c
+                        nc.tensor.matmul_mx(
+                            out=mx1[:, c, :],
+                            lhsT=wt[b][:, g, byte : byte + 256].bitcast(FP4X4),
+                            lhsT_scale=scale,
+                            rhs=xc[:, g, P * a : P * (a + 1)].bitcast(FP8X4),
+                            rhs_scale=xcs[:, g, P * a : P * (a + 1)],
+                            start=(g == 0),
+                            stop=(g == G - 1),
+                        )
+            quad, j = divmod(n - MX2_LAG, 4)
+            us = []
+            if n >= MX2_LAG and quad < units // 4:
+                for st in (2 * j, 2 * j + 1):
+                    u_ps = psum.tile([P, 512], F32, name="u_ps", tag="u", bufs=2)
+                    nc.tensor.matmul_mx(
+                        out=u_ps[:],
+                        lhsT=kc[:, 512 * st : 512 * (st + 1)].bitcast(FP8X4),
+                        lhsT_scale=ksc[:, P * st : P * (st + 1)],
+                        rhs=zc_of[quad][:].bitcast(FP8X4),
+                        rhs_scale=zs_of[quad][:],
+                        start=True,
+                        stop=True,
+                    )
+                    us.append((st, u_ps))
+
+            m = n - 2
+            if 0 <= m < units:
+                a = m // H
+                t1 = t1_of[m]
+                rinv = rinv_of[m]
+                pp = work.tile([P, D], F32, name="pp", tag="pp")
+                qq = work.tile([P, D], F32, name="qq", tag="qq")
+                nc.vector.scalar_tensor_tensor(
+                    out=pp[:], in0=t1[:], scalar=rinv[:], in1=cos_d[:, a, :, :].rearrange("p r e -> p (r e)"),
+                    op0=ALU.mult, op1=ALU.mult,
+                )
+                nc.vector.scalar_tensor_tensor(
+                    out=qq[:].rearrange("p (r e) -> p r e", e=2),
+                    in0=t1[:].rearrange("p (r e) -> p r e", e=2)[:, :, ::-1],
+                    scalar=rinv[:],
+                    in1=sin_s[:, a, :, :],
+                    op0=ALU.mult, op1=ALU.mult,
+                )
+                z = work.tile([P, D], BF16, name="z", tag="z", align_bytes=64)
+                nc.gpsimd.tensor_tensor(
+                    out=z[:].rearrange("i (u p e) -> i u p e", u=2, e=2),
+                    in0=pp[:].rearrange("i (p u e) -> i u p e", u=2, e=2),
+                    in1=qq[:].rearrange("i (p u e) -> i u p e", u=2, e=2),
+                    op=ALU.add,
+                )
+                z_of[m] = z
+
+            vs = []
+            for st, u_ps in us:
+                v = work.tile([P, 512], F32, name="v", tag="v", bufs=6)
+                qa, qb = divmod(quad, NQ)
+                nc.vector.scalar_tensor_tensor(
+                    out=v[:], in0=u_ps[:], scalar=nkb[:, st : st + 1],
+                    in1=alpha_t[:, qa, 4 * qb : 4 * qb + 4, :].rearrange("p h i -> p (h i)"),
+                    op0=ALU.max, op1=ALU.mult,
+                )
+                vs.append((quad, st, v))
+            v_of[n] = vs
+
+            if n < units:
+                h = n % H
+                yg = work.tile([P, 4, P], F32, name="yg", tag="yg")
+                sq = work.tile([P, 4, P], F32, name="sq", tag="sq")
+                for c in range(4):
+                    k = 4 * h + c
+                    nc.scalar.activation(out=sq[:, c, :], in_=mx1[:, c, :], func=ACT.Square, bias=bcol[:, k : k + 1])
+                    nc.scalar.activation(
+                        out=yg[:, c, :], in_=mx1[:, c, :], func=ACT.Identity,
+                        bias=gbcol[:, k : k + 1], scale=gcol[:, k : k + 1],
+                    )
+                yg_of[n], sq_of[n] = yg, sq
+
+            for pq, st, v in v_of.get(n - 1, []):
+                qa, qb = divmod(pq, NQ)
+                half, sc = divmod(st, 4)
+                if qb == 0 and sc == 0:
+                    acc[half] = psum.tile([P, 512], F32, name=f"acc{half}", tag=f"acc{half}", bufs=1)
+                for hh in range(4):
+                    nc.tensor.matmul(
+                        acc[half][:, P * sc : P * (sc + 1)], lhsT=v[:, P * hh : P * (hh + 1)], rhs=ident[:],
+                        is_transpose=True,
+                        start=(qb == 0 and sc == 0 and hh == 0),
+                        stop=(qb == NQ - 1 and sc == 3 and hh == 3),
+                    )
+                if qb == NQ - 1 and sc == 3:
+                    o = work.tile([P, 512], F32, name="o", tag="o", bufs=2)
+                    nc.vector.scalar_tensor_tensor(
+                        out=o[:], in0=kb_all[:, 512 * half : 512 * (half + 1)], scalar=asum4[:, qa : qa + 1],
+                        in1=acc[half][:], op0=ALU.mult, op1=ALU.add,
+                    )
+                    nc.sync.dma_start(out=out[P * qa : P * (qa + 1), 512 * half : 512 * (half + 1)], in_=o[:])
+            mt, mz = n - 1, n - 3
+            if 0 <= mt < units or 0 <= mz < units:
+                misc = psum.tile([P, 4, P], F32, name="misc", tag="misc", bufs=1)
+            if 0 <= mt < units:
+                t1 = psum.tile([P, D], F32, name="t1", tag="t1", bufs=2)
+                for c in range(4):
+                    nc.tensor.transpose(t1[:, P * c : P * (c + 1)], yg_of[mt][:, c, :], ident[:])
+                t1_of[mt] = t1
+            if 0 <= mz < units:
+                words = z_of[mz][:].bitcast(F32)
+                for u in range(2):
+                    nc.tensor.transpose(misc[:, 1 + u, :], words[:, P * u : P * (u + 1)], ident[:])
+            if 0 <= mt < units:
+                for c in range(4):
+                    nc.tensor.matmul(
+                        misc[:, 0, :], lhsT=sq_of[mt][:, c, :], rhs=ident[:], is_transpose=True,
+                        start=(c == 0), stop=(c == 3),
+                    )
+                ss = work.tile([P, 1], F32, name="ss", tag="ss")
+                junk = work.tile([P, P], F32, name="junk", tag="junk", bufs=2)
+                nc.scalar.activation(out=junk[:], in_=misc[:, 0, :], func=ACT.Identity, accum_out=ss[:])
+                rms = work.tile([P, 1], F32, name="rms", tag="rms")
+                nc.scalar.activation(out=rms[:], in_=ss[:], func=ACT.Sqrt, scale=1.0 / D)
+                rinv = work.tile([P, 1], F32, name="rinv", tag="rinv")
+                nc.vector.reciprocal(out=rinv[:], in_=rms[:])
+                rinv_of[mt] = rinv
+            if 0 <= mz < units:
+                zq, zi = divmod(mz, 4)
+                if zi == 0:
+                    grp = work.tile([P, 4, P * 4], BF16, name="grp", tag="grp", bufs=2, align_bytes=64)
+                    grp_of[zq] = grp
+                nc.scalar.copy(
+                    out=grp_of[zq][:, zi, :].bitcast(F32).rearrange("p (i u) -> p i u", u=2),
+                    in_=misc[:, 1:3, :].rearrange("p u i -> p i u"),
+                )
+                if zi == 3:
+                    zc = work.tile([P, 512], U32, name="zc", tag="zc", bufs=2, align_bytes=64)
+                    zs = work.tile([P, 512], U8, name="zs", tag="zs", bufs=2, align_bytes=64)
+                    nc.vector.quantize_mx(
+                        out=zc[:].bitcast(FP8X4), scales=zs[:], in_=grp_of[zq][:].rearrange("p n k -> p (n k)")
+                    )
+                    zc_of[zq], zs_of[zq] = zc, zs

@@ -23,7 +23,7 @@ G = E // 512
 NA = T // P
 NQ = 4
 ROOT_D = math.sqrt(D)
-MX2_LAG = 7
+MX2_LAG = 8
 
 
 def tile_shared_key_index_scores_f7_kernel(
@@ -43,54 +43,59 @@ def tile_shared_key_index_scores_f7_kernel(
         nc.scalar.dma_start(out=gb_rows[0:64, :], in_=gain.rearrange("h (c m) -> (h c) m", m=P))
         nc.scalar.dma_start(out=gb_rows[64:128, :], in_=bias.rearrange("(c m) -> c m", m=P))
 
-        xb = keep.tile([P, NA, E], U8, name="xb", align_bytes=64)
-        nc.sync.dma_start(out=xb[:], in_=x_bytes.rearrange("(a p) k -> p a k", p=P))
+        xb = []
+        for a in range(NA):
+            x_raw = keep.tile([P, E], U8, name=f"xb{a}", align_bytes=64)
+            xb.append(x_raw)
+        nc.sync.dma_start(out=xb[0][:], in_=x_bytes[0:P, :])
         xs = keep.tile([P, E], F32, name="xs")
         nc.sync.dma_start(out=xs[:], in_=x_scale.rearrange("o k -> (o k)").partition_broadcast(P))
 
-        wsc0 = keep.tile([P, G, 2048], U8, name="wsc0", align_bytes=64)
-        wscr = keep.tile([P, G, 6144], U8, name="wscr", align_bytes=64)
+        wsc = []
+        for b in range(NQ):
+            ws = keep.tile([P, G, 2048], U8, name=f"wsc{b}", align_bytes=64)
+            wsc.append(ws)
         ksc = keep.tile([P, S], U8, name="ksc", align_bytes=64)
         kb_rows = keep.tile([P, P], BF16, name="kb_rows")
-        nc.vector.memset(wsc0[:].rearrange("p g n -> p (g n)").bitcast(I32), 0)
+        nc.vector.memset(wsc[0][:].rearrange("p g n -> p (g n)").bitcast(I32), 0)
         nc.vector.memset(kb_rows[:], 0.0)
-        nc.vector.memset(wscr[:].rearrange("p g n -> p (g n)").bitcast(I32), 0)
+        nc.vector.memset(wsc[1][:].rearrange("p g n -> p (g n)").bitcast(I32), 0)
         nc.vector.memset(ksc[:].bitcast(I32), 0)
+        nc.vector.memset(wsc[2][:].rearrange("p g n -> p (g n)").bitcast(I32), 0)
+        nc.vector.memset(wsc[3][:].rearrange("p g n -> p (g n)").bitcast(I32), 0)
 
         nc.scalar.dma_start(out=kb_rows[0:8, :], in_=key_bias.rearrange("(c m) -> c m", m=P))
-        for q in range(4):
-            nc.sync.dma_start(
-                out=wsc0[32 * q : 32 * q + 4, :, :].bitcast(I32),
-                in_=wq_scales[:, 4 * q : 4 * q + 4, 0:2048].rearrange("g r n -> r g n").bitcast(I32),
-            )
         wt = []
         for b in range(NQ):
             w = keep.tile([P, G, 4096], U8, name=f"w{b}", align_bytes=64)
             wt.append(w)
-        nc.sync.dma_start(out=wt[0][:], in_=wq_words[:, :, 0:4096].rearrange("g p n -> p g n"))
         cs = keep.tile([P, NA, D // 2], BF16, name="cs")
         sn = keep.tile([P, NA, D // 2], BF16, name="sn")
+        kc = keep.tile([P, 4 * S], U8, name="kc", align_bytes=64)
+        kb_all = keep.tile([P, S], BF16, name="kb_all")
+
+        def load_weights(b):
+            for q in range(4):
+                nc.sync.dma_start(
+                    out=wsc[b][32 * q : 32 * q + 4, :, :].bitcast(I32),
+                    in_=wq_scales[:, 4 * q : 4 * q + 4, 2048 * b : 2048 * (b + 1)].rearrange("g r n -> r g n").bitcast(I32),
+                )
+            nc.sync.dma_start(out=wt[b][:], in_=wq_words[:, :, 4096 * b : 4096 * (b + 1)].rearrange("g p n -> p g n"))
+
+        load_weights(0)
+        nc.sync.dma_start(out=xb[1][:], in_=x_bytes[P : 2 * P, :])
         nc.sync.dma_start(out=cs[:], in_=cosines.rearrange("(a p) r -> p a r", p=P))
         nc.sync.dma_start(out=sn[:], in_=sines.rearrange("(a p) r -> p a r", p=P))
-        for q in range(4):
-            nc.sync.dma_start(
-                out=wscr[32 * q : 32 * q + 4, :, :].bitcast(I32),
-                in_=wq_scales[:, 4 * q : 4 * q + 4, 2048:8192].rearrange("g r n -> r g n").bitcast(I32),
-            )
-        nc.sync.dma_start(out=wt[1][:], in_=wq_words[:, :, 4096:8192].rearrange("g p n -> p g n"))
+        load_weights(1)
         for q in range(4):
             nc.sync.dma_start(
                 out=ksc[32 * q : 32 * q + 4, :].bitcast(I32),
                 in_=k_scales[0, 4 * q : 4 * q + 4, :].bitcast(I32),
             )
-        kc = keep.tile([P, 4 * S], U8, name="kc", align_bytes=64)
         nc.sync.dma_start(out=kc[:], in_=k_words[0].rearrange("p n t -> p (n t)"))
-        kb_all = keep.tile([P, S], BF16, name="kb_all")
+        load_weights(2)
+        load_weights(3)
         nc.sync.dma_start(out=kb_all[:], in_=key_bias.partition_broadcast(P))
-        for b in range(2, NQ):
-            nc.sync.dma_start(
-                out=wt[b][:], in_=wq_words[:, :, 4096 * b : 4096 * (b + 1)].rearrange("g p n -> p g n")
-            )
 
         ident = keep.tile([P, P], F32, name="ident")
         make_identity(nc, ident[:])
@@ -106,7 +111,7 @@ def tile_shared_key_index_scores_f7_kernel(
         asum4 = keep.tile([P, NA], F32, name="asum4")
         nc.vector.tensor_scalar(out=asum4[:], in0=asum[:], scalar1=0.25, scalar2=None, op0=ALU.mult)
         warm = keep.tile([P, 1], F32, name="warm")
-        nc.scalar.activation(out=warm[:], in_=asum[:, 0:1], func=ACT.Sqrt)
+        nc.scalar.activation(out=warm[:], in_=asum[:, 0:1], func=ACT.Abs_reciprocal_sqrt)
 
         cols_ps = psum.tile([P, 2, P], BF16, name="cols_ps", tag="u", bufs=2)
         nc.tensor.transpose(cols_ps[:, 0, :], gb_rows[:], identb[:])
@@ -121,13 +126,13 @@ def tile_shared_key_index_scores_f7_kernel(
         nc.vector.tensor_tensor(out=gbcol[:], in0=gcol[:], in1=bcol[:], op=ALU.mult)
 
         alpha_t = keep.tile([P, NA, H, P], F32, name="alpha_t")
-        for a in range(NA):
-            for b in range(NQ):
-                at_ps = psum.tile([P, 4, P], F32, name="at_ps", tag="u", bufs=2)
-                for hh in range(4):
-                    h = 4 * b + hh
-                    nc.tensor.transpose(at_ps[:, hh, :], alpha_s[:, a, h : h + 1].to_broadcast([P, P]), ident[:])
-                nc.scalar.copy(out=alpha_t[:, a, 4 * b : 4 * b + 4, :], in_=at_ps[:])
+
+        def spread_gates(a, b):
+            at_ps = psum.tile([P, 4, P], F32, name="at_ps", tag="u", bufs=2)
+            for hh in range(4):
+                h = 4 * b + hh
+                nc.tensor.transpose(at_ps[:, hh, :], alpha_s[:, a, h : h + 1].to_broadcast([P, P]), ident[:])
+            return at_ps
 
         cos_d = keep.tile([P, NA, D // 2, 2], BF16, name="cos_d")
         sin_s = keep.tile([P, NA, D // 2, 2], BF16, name="sin_s")
@@ -138,23 +143,33 @@ def tile_shared_key_index_scores_f7_kernel(
                 nc.gpsimd.tensor_scalar(out=sin_s[:, a, :, e], in0=sn[:, a, :], scalar1=sign, scalar2=0.0, op0=ALU.mult, op1=ALU.add)
 
         xp = keep.tile([P, NA, E], BF16, name="xp", align_bytes=64)
-        for a in range(NA):
-            nc.vector.tensor_tensor(out=xp[:, a, :], in0=xb[:, a, :].bitcast(FP8), in1=xs[:], op=ALU.mult)
-        xc = keep.tile([P, G, T], U32, name="xc", align_bytes=64)
-        xcs = keep.tile([P, G, T], U8, name="xcs", align_bytes=64)
-        xg = keep.tile([P, G, T * 4], BF16, name="xg", align_bytes=64)
-        for g in range(G):
-            xt_ps = psum.tile([P, NA, 2, P], F32, name="xt_ps", tag="t1", bufs=2)
-            for a in range(NA):
-                words = xp[:, a, :].bitcast(F32)
+        xc = keep.tile([P, NA, G, P], U32, name="xc", align_bytes=64)
+        xcs = keep.tile([P, NA, G, P], U8, name="xcs", align_bytes=64)
+        xg = keep.tile([P, NA, G * P * 4], BF16, name="xg", align_bytes=64)
+
+        def x_turned(a):
+            nc.vector.tensor_tensor(out=xp[:, a, :], in0=xb[a][:].bitcast(FP8), in1=xs[:], op=ALU.mult)
+            words = xp[:, a, :].bitcast(F32)
+            xt_ps = psum.tile([P, G, 2, P], F32, name="xt_ps", tag="t1", bufs=2)
+            for g in range(G):
                 for u in range(2):
-                    nc.tensor.transpose(xt_ps[:, a, u, :], words[:, 256 * g + u : 256 * (g + 1) : 2], ident[:])
+                    nc.tensor.transpose(xt_ps[:, g, u, :], words[:, 256 * g + u : 256 * (g + 1) : 2], ident[:])
+            return xt_ps
+
+        def x_quantized(a, xt_ps):
             nc.vector.tensor_copy(
-                out=xg[:, g, :].bitcast(F32).rearrange("p (a i u) -> p a i u", a=NA, u=2),
-                in_=xt_ps[:].rearrange("p a u i -> p a i u"),
+                out=xg[:, a, :].bitcast(F32).rearrange("p (g i u) -> p g i u", g=G, u=2),
+                in_=xt_ps[:].rearrange("p g u i -> p g i u"),
             )
-        for g in range(G):
-            nc.vector.quantize_mx(out=xc[:, g, :].bitcast(FP8X4), scales=xcs[:, g, :], in_=xg[:, g, :])
+            nc.vector.quantize_mx(
+                out=xc[:, a, :, :].rearrange("p g i -> p (g i)").bitcast(FP8X4),
+                scales=xcs[:, a, :, :].rearrange("p g i -> p (g i)"), in_=xg[:, a, :],
+            )
+
+        for b in range(NQ):
+            at_ps = spread_gates(0, b)
+            nc.scalar.copy(out=alpha_t[:, 0, 4 * b : 4 * b + 4, :], in_=at_ps[:])
+        x_quantized(0, x_turned(0))
 
         units = NA * H
         yg_of, sq_of, t1_of, rinv_of, pq_of, z_of = {}, {}, {}, {}, {}, {}
@@ -165,21 +180,17 @@ def tile_shared_key_index_scores_f7_kernel(
             if n < units:
                 a, h = divmod(n, H)
                 b, hq = divmod(h, 4)
-                mx1 = psum.tile([P, 4, P], F32, name="mx1", tag="mx1", bufs=1)
+                mx1 = psum.tile([P, 4, P], F32, name="mx1", tag=("mx1", "acc0", "acc1")[n % 3] if n < 8 else "mx1", bufs=1)
                 for c in range(4):
                     for g in range(G):
-                        if b == 0:
-                            scale = wsc0[:, g, 512 * hq + P * c : 512 * hq + P * (c + 1)]
-                        else:
-                            col = 512 * (h - 4) + P * c
-                            scale = wscr[:, g, col : col + P]
+                        scale = wsc[b][:, g, 512 * hq + P * c : 512 * hq + P * (c + 1)]
                         byte = 1024 * hq + 256 * c
                         nc.tensor.matmul_mx(
                             out=mx1[:, c, :],
                             lhsT=wt[b][:, g, byte : byte + 256].bitcast(FP4X4),
                             lhsT_scale=scale,
-                            rhs=xc[:, g, P * a : P * (a + 1)].bitcast(FP8X4),
-                            rhs_scale=xcs[:, g, P * a : P * (a + 1)],
+                            rhs=xc[:, a, g, :].bitcast(FP8X4),
+                            rhs_scale=xcs[:, a, g, :],
                             start=(g == 0),
                             stop=(g == G - 1),
                         )
@@ -217,14 +228,6 @@ def tile_shared_key_index_scores_f7_kernel(
                     in1=sin_s[:, a, :, :],
                     op0=ALU.mult, op1=ALU.mult,
                 )
-                z = work.tile([P, D], BF16, name="z", tag="z", align_bytes=64)
-                nc.gpsimd.tensor_tensor(
-                    out=z[:].rearrange("i (u p e) -> i u p e", u=2, e=2),
-                    in0=pp[:].rearrange("i (p u e) -> i u p e", u=2, e=2),
-                    in1=qq[:].rearrange("i (p u e) -> i u p e", u=2, e=2),
-                    op=ALU.add,
-                )
-                z_of[m] = z
 
             vs = []
             for st, u_ps in us:
@@ -237,6 +240,15 @@ def tile_shared_key_index_scores_f7_kernel(
                 )
                 vs.append((quad, st, v))
             v_of[n] = vs
+            if 0 <= m < units:
+                z = work.tile([P, D], BF16, name="z", tag="z", align_bytes=64)
+                nc.vector.tensor_tensor(
+                    out=z[:].rearrange("i (u p e) -> i u p e", u=2, e=2),
+                    in0=pp[:].rearrange("i (p u e) -> i u p e", u=2, e=2),
+                    in1=qq[:].rearrange("i (p u e) -> i u p e", u=2, e=2),
+                    op=ALU.add,
+                )
+                z_of[m] = z
 
             if n < units:
                 h = n % H
@@ -245,12 +257,24 @@ def tile_shared_key_index_scores_f7_kernel(
                 for c in range(4):
                     k = 4 * h + c
                     nc.scalar.activation(out=sq[:, c, :], in_=mx1[:, c, :], func=ACT.Square, bias=bcol[:, k : k + 1])
-                    nc.scalar.activation(
-                        out=yg[:, c, :], in_=mx1[:, c, :], func=ACT.Identity,
-                        bias=gbcol[:, k : k + 1], scale=gcol[:, k : k + 1],
-                    )
+                for c in range(4):
+                    k = 4 * h + c
+                    if n < 8 and c >= 2:
+                        nc.vector.tensor_scalar(
+                            out=yg[:, c, :], in0=mx1[:, c, :], scalar1=gcol[:, k : k + 1], scalar2=gbcol[:, k : k + 1],
+                            op0=ALU.mult, op1=ALU.add,
+                        )
+                    else:
+                        nc.scalar.activation(
+                            out=yg[:, c, :], in_=mx1[:, c, :], func=ACT.Identity,
+                            bias=gbcol[:, k : k + 1], scale=gcol[:, k : k + 1],
+                        )
                 yg_of[n], sq_of[n] = yg, sq
 
+            gates = []
+            if 1 <= n < 5:
+                ab = (1, n - 1)
+                gates.append((ab, spread_gates(*ab)))
             for pq, st, v in v_of.get(n - 1, []):
                 qa, qb = divmod(pq, NQ)
                 half, sc = divmod(st, 4)
@@ -291,10 +315,8 @@ def tile_shared_key_index_scores_f7_kernel(
                 ss = work.tile([P, 1], F32, name="ss", tag="ss")
                 junk = work.tile([P, P], F32, name="junk", tag="junk", bufs=2)
                 nc.scalar.activation(out=junk[:], in_=misc[:, 0, :], func=ACT.Identity, accum_out=ss[:])
-                rms = work.tile([P, 1], F32, name="rms", tag="rms")
-                nc.scalar.activation(out=rms[:], in_=ss[:], func=ACT.Sqrt, scale=1.0 / D)
-                rinv = work.tile([P, 1], F32, name="rinv", tag="rinv")
-                nc.vector.reciprocal(out=rinv[:], in_=rms[:])
+                rinv = work.tile([P, 1], F32, name="rinv", tag="rinv", bufs=4)
+                nc.scalar.activation(out=rinv[:], in_=ss[:], func=ACT.Abs_reciprocal_sqrt, scale=1.0 / D)
                 rinv_of[mt] = rinv
             if 0 <= mz < units:
                 zq, zi = divmod(mz, 4)
@@ -312,3 +334,7 @@ def tile_shared_key_index_scores_f7_kernel(
                         out=zc[:].bitcast(FP8X4), scales=zs[:], in_=grp_of[zq][:].rearrange("p n k -> p (n k)")
                     )
                     zc_of[zq], zs_of[zq] = zc, zs
+            for (ga, gb), at_ps in gates:
+                nc.scalar.copy(out=alpha_t[:, ga, 4 * gb : 4 * gb + 4, :], in_=at_ps[:])
+            if n == 0:
+                x_quantized(1, x_turned(1))

@@ -23,7 +23,6 @@ G = E // 512
 NA = T // P
 NQ = 4
 ROOT_D = math.sqrt(D)
-MX2_LAG = 8
 
 
 def tile_shared_key_index_scores_f7_kernel(
@@ -37,19 +36,23 @@ def tile_shared_key_index_scores_f7_kernel(
         psum = ctx.enter_context(tc.psum_pool(name="psum", bufs=1))
         ctx.enter_context(tc.manual_schedule())
 
-        hg = keep.tile([P, NA, H], BF16, name="hg")
-        nc.scalar.dma_start(out=hg[:], in_=head_gate.rearrange("(a p) h -> p a h", p=P))
         gb_rows = keep.tile([P, P], BF16, name="gb_rows")
         nc.scalar.dma_start(out=gb_rows[0:64, :], in_=gain.rearrange("h (c m) -> (h c) m", m=P))
         nc.scalar.dma_start(out=gb_rows[64:128, :], in_=bias.rearrange("(c m) -> c m", m=P))
+        hg = keep.tile([P, NA, H], BF16, name="hg")
+        nc.scalar.dma_start(out=hg[:], in_=head_gate.rearrange("(a p) h -> p a h", p=P))
 
         xb = []
         for a in range(NA):
             x_raw = keep.tile([P, E], U8, name=f"xb{a}", align_bytes=64)
             xb.append(x_raw)
+        xs = []
+        for g in range(G):
+            xs_half = keep.tile([P, 512], F32, name=f"xs{g}")
+            xs.append(xs_half)
         nc.sync.dma_start(out=xb[0][:], in_=x_bytes[0:P, :])
-        xs = keep.tile([P, E], F32, name="xs")
-        nc.sync.dma_start(out=xs[:], in_=x_scale.rearrange("o k -> (o k)").partition_broadcast(P))
+        for g in range(G):
+            nc.sync.dma_start(out=xs[g][:], in_=x_scale[0, 512 * g : 512 * (g + 1)].partition_broadcast(P))
 
         wsc = []
         for b in range(NQ):
@@ -63,12 +66,16 @@ def tile_shared_key_index_scores_f7_kernel(
         nc.vector.memset(ksc[:].bitcast(I32), 0)
         nc.vector.memset(wsc[2][:].rearrange("p g n -> p (g n)").bitcast(I32), 0)
         nc.vector.memset(wsc[3][:].rearrange("p g n -> p (g n)").bitcast(I32), 0)
-
         nc.scalar.dma_start(out=kb_rows[0:8, :], in_=key_bias.rearrange("(c m) -> c m", m=P))
-        wt = []
-        for b in range(NQ):
+
+        wt = [None]
+        for b in range(1, NQ):
             w = keep.tile([P, G, 4096], U8, name=f"w{b}", align_bytes=64)
             wt.append(w)
+        w_first = []
+        for h in range(4):
+            w = keep.tile([P, G, 1024], U8, name=f"wf{h}", align_bytes=64)
+            w_first.append(w)
         cs = keep.tile([P, NA, D // 2], BF16, name="cs")
         sn = keep.tile([P, NA, D // 2], BF16, name="sn")
         kc = keep.tile([P, 4 * S], U8, name="kc", align_bytes=64)
@@ -80,12 +87,15 @@ def tile_shared_key_index_scores_f7_kernel(
                     out=wsc[b][32 * q : 32 * q + 4, :, :].bitcast(I32),
                     in_=wq_scales[:, 4 * q : 4 * q + 4, 2048 * b : 2048 * (b + 1)].rearrange("g r n -> r g n").bitcast(I32),
                 )
-            nc.sync.dma_start(out=wt[b][:], in_=wq_words[:, :, 4096 * b : 4096 * (b + 1)].rearrange("g p n -> p g n"))
+            for h in range(4 * b, 4 * b + 4) if b == 0 else ():
+                nc.sync.dma_start(out=w_first[h][:], in_=wq_words[:, :, 1024 * h : 1024 * (h + 1)].rearrange("g p n -> p g n"))
+            if b:
+                nc.sync.dma_start(out=wt[b][:], in_=wq_words[:, :, 4096 * b : 4096 * (b + 1)].rearrange("g p n -> p g n"))
 
         load_weights(0)
-        nc.sync.dma_start(out=xb[1][:], in_=x_bytes[P : 2 * P, :])
         nc.sync.dma_start(out=cs[:], in_=cosines.rearrange("(a p) r -> p a r", p=P))
         nc.sync.dma_start(out=sn[:], in_=sines.rearrange("(a p) r -> p a r", p=P))
+        nc.sync.dma_start(out=xb[1][:], in_=x_bytes[P : 2 * P, :])
         load_weights(1)
         for q in range(4):
             nc.sync.dma_start(
@@ -102,17 +112,6 @@ def tile_shared_key_index_scores_f7_kernel(
         identb = keep.tile([P, P], BF16, name="identb")
         make_identity(nc, identb[:])
 
-        alpha = keep.tile([P, NA, H], F32, name="alpha")
-        asum = keep.tile([P, NA], F32, name="asum")
-        for a in range(NA):
-            nc.scalar.activation(out=alpha[:, a, :], in_=hg[:, a, :], func=ACT.Sigmoid, accum_out=asum[:, a : a + 1])
-        alpha_s = keep.tile([P, NA, H], F32, name="alpha_s")
-        nc.vector.tensor_scalar(out=alpha_s[:], in0=alpha[:], scalar1=1.0 / (4.0 * ROOT_D), scalar2=None, op0=ALU.mult)
-        asum4 = keep.tile([P, NA], F32, name="asum4")
-        nc.vector.tensor_scalar(out=asum4[:], in0=asum[:], scalar1=0.25, scalar2=None, op0=ALU.mult)
-        warm = keep.tile([P, 1], F32, name="warm")
-        nc.scalar.activation(out=warm[:], in_=asum[:, 0:1], func=ACT.Abs_reciprocal_sqrt)
-
         cols_ps = psum.tile([P, 2, P], BF16, name="cols_ps", tag="u", bufs=2)
         nc.tensor.transpose(cols_ps[:, 0, :], gb_rows[:], identb[:])
         nc.tensor.transpose(cols_ps[:, 1, :], kb_rows[:], identb[:])
@@ -120,11 +119,56 @@ def tile_shared_key_index_scores_f7_kernel(
         bcol = keep.tile([P, 64], F32, name="bcol")
         gbcol = keep.tile([P, 64], F32, name="gbcol")
         nkb = keep.tile([P, 8], F32, name="nkb")
+        pkb = keep.tile([P, 8], F32, name="pkb")
         nc.vector.tensor_copy(out=gcol[:], in_=cols_ps[:, 0, 0:64])
         nc.vector.tensor_copy(out=bcol[:], in_=cols_ps[:, 0, 64:128])
         nc.vector.tensor_scalar(out=nkb[:], in0=cols_ps[:, 1, 0:8], scalar1=-ROOT_D, scalar2=None, op0=ALU.mult)
+        nc.vector.tensor_scalar(out=pkb[:], in0=cols_ps[:, 1, 0:8], scalar1=ROOT_D, scalar2=None, op0=ALU.mult)
         nc.vector.tensor_tensor(out=gbcol[:], in0=gcol[:], in1=bcol[:], op=ALU.mult)
+        xp = keep.tile([P, NA, G, 512], BF16, name="xp", align_bytes=64)
+        xc = keep.tile([P, NA, G, P], U32, name="xc", align_bytes=64)
+        xcs = keep.tile([P, NA, G, P], U8, name="xcs", align_bytes=64)
+        xg = keep.tile([P, NA, G, P * 4], BF16, name="xg", align_bytes=64)
 
+        def x_scaled(a):
+            for g in range(G):
+                nc.vector.tensor_tensor(out=xp[:, a, g, :], in0=xb[a][:, 512 * g : 512 * (g + 1)].bitcast(FP8), in1=xs[g][:], op=ALU.mult)
+
+        def x_turned(a):
+            turned = []
+            for g in range(G):
+                words = xp[:, a, g, :].bitcast(F32)
+                xt_ps = psum.tile([P, 2, P], F32, name="xt_ps", tag=f"acc{g}", bufs=1)
+                for u in range(2):
+                    nc.tensor.transpose(xt_ps[:, u, :], words[:, u::2], ident[:])
+                turned.append(xt_ps)
+            return turned
+
+        def x_quantized(a, turned):
+            for g in range(G):
+                nc.vector.tensor_copy(
+                    out=xg[:, a, g, :].bitcast(F32).rearrange("p (i u) -> p i u", u=2),
+                    in_=turned[g][:].rearrange("p u i -> p i u"),
+                )
+            nc.vector.quantize_mx(
+                out=xc[:, a, :, :].rearrange("p g i -> p (g i)").bitcast(FP8X4),
+                scales=xcs[:, a, :, :].rearrange("p g i -> p (g i)"), in_=xg[:, a, :, :].rearrange("p g k -> p (g k)"),
+            )
+
+        x_scaled(0)
+        xt0 = x_turned(0)
+        x_quantized(0, xt0)
+
+        alpha = keep.tile([P, NA, H], F32, name="alpha")
+        asum = keep.tile([P, NA], F32, name="asum")
+        for a in range(NA):
+            nc.scalar.activation(out=alpha[:, a, :], in_=hg[:, a, :], func=ACT.Sigmoid, accum_out=asum[:, a : a + 1])
+        warm = keep.tile([P, 1], F32, name="warm")
+        nc.scalar.activation(out=warm[:], in_=asum[:, 0:1], func=ACT.Abs_reciprocal_sqrt)
+        alpha_s = keep.tile([P, NA, H], F32, name="alpha_s")
+        nc.vector.tensor_scalar(out=alpha_s[:], in0=alpha[:], scalar1=1.0 / (4.0 * ROOT_D), scalar2=None, op0=ALU.mult)
+        asum4 = keep.tile([P, NA], F32, name="asum4")
+        nc.vector.tensor_scalar(out=asum4[:], in0=asum[:], scalar1=0.25, scalar2=None, op0=ALU.mult)
         alpha_t = keep.tile([P, NA, H, P], F32, name="alpha_t")
 
         def spread_gates(a, b):
@@ -134,121 +178,116 @@ def tile_shared_key_index_scores_f7_kernel(
                 nc.tensor.transpose(at_ps[:, hh, :], alpha_s[:, a, h : h + 1].to_broadcast([P, P]), ident[:])
             return at_ps
 
-        cos_d = keep.tile([P, NA, D // 2, 2], BF16, name="cos_d")
-        sin_s = keep.tile([P, NA, D // 2, 2], BF16, name="sin_s")
+        tab = keep.tile([P, NA, D // 2, 4], BF16, name="tab")
         for a in range(NA):
-            for e in range(2):
-                nc.gpsimd.tensor_scalar(out=cos_d[:, a, :, e], in0=cs[:, a, :], scalar1=1.0, scalar2=0.0, op0=ALU.mult, op1=ALU.add)
-                sign = 1.0 if e else -1.0
-                nc.gpsimd.tensor_scalar(out=sin_s[:, a, :, e], in0=sn[:, a, :], scalar1=sign, scalar2=0.0, op0=ALU.mult, op1=ALU.add)
-
-        xp = keep.tile([P, NA, E], BF16, name="xp", align_bytes=64)
-        xc = keep.tile([P, NA, G, P], U32, name="xc", align_bytes=64)
-        xcs = keep.tile([P, NA, G, P], U8, name="xcs", align_bytes=64)
-        xg = keep.tile([P, NA, G * P * 4], BF16, name="xg", align_bytes=64)
-
-        def x_turned(a):
-            nc.vector.tensor_tensor(out=xp[:, a, :], in0=xb[a][:].bitcast(FP8), in1=xs[:], op=ALU.mult)
-            words = xp[:, a, :].bitcast(F32)
-            xt_ps = psum.tile([P, G, 2, P], F32, name="xt_ps", tag="t1", bufs=2)
-            for g in range(G):
-                for u in range(2):
-                    nc.tensor.transpose(xt_ps[:, g, u, :], words[:, 256 * g + u : 256 * (g + 1) : 2], ident[:])
-            return xt_ps
-
-        def x_quantized(a, xt_ps):
-            nc.vector.tensor_copy(
-                out=xg[:, a, :].bitcast(F32).rearrange("p (g i u) -> p g i u", g=G, u=2),
-                in_=xt_ps[:].rearrange("p g u i -> p g i u"),
-            )
-            nc.vector.quantize_mx(
-                out=xc[:, a, :, :].rearrange("p g i -> p (g i)").bitcast(FP8X4),
-                scales=xcs[:, a, :, :].rearrange("p g i -> p (g i)"), in_=xg[:, a, :],
-            )
-
-        for b in range(NQ):
-            at_ps = spread_gates(0, b)
-            nc.scalar.copy(out=alpha_t[:, 0, 4 * b : 4 * b + 4, :], in_=at_ps[:])
-        x_quantized(0, x_turned(0))
+            for j, (src, sign) in enumerate(((cs, 1.0), (sn, 1.0), (sn, -1.0), (cs, 1.0))):
+                nc.gpsimd.tensor_scalar(out=tab[:, a, :, j], in0=src[:, a, :], scalar1=sign, scalar2=0.0, op0=ALU.mult, op1=ALU.add)
 
         units = NA * H
-        yg_of, sq_of, t1_of, rinv_of, pq_of, z_of = {}, {}, {}, {}, {}, {}
+        yg_of, sq_of, t1_of, rinv_of, z_of = {}, {}, {}, {}, {}
         grp_of, zc_of, zs_of, v_of = {}, {}, {}, {}
         acc = {}
-        misc = None
-        for n in range(units + MX2_LAG + 2):
+        ready = []
+        groups = []
+        for size in [4] * 8:
+            first = groups[-1][0] + groups[-1][1] if groups else 0
+            groups.append((first, size))
+        group_of = {first + k: (j, k) for j, (first, size) in enumerate(groups) for k in range(size)}
+        todo = []
+        for j, (first, size) in enumerate(groups):
+            step = 4 // size
+            todo.extend((j, range(st, st + step)) for st in range(0, 8, step))
+        n = 0
+        busy = True
+        while busy:
             if n < units:
                 a, h = divmod(n, H)
                 b, hq = divmod(h, 4)
-                mx1 = psum.tile([P, 4, P], F32, name="mx1", tag=("mx1", "acc0", "acc1")[n % 3] if n < 8 else "mx1", bufs=1)
+                mx1 = psum.tile([P, 4, P], F32, name="mx1", tag="mx1", bufs=2)
                 for c in range(4):
                     for g in range(G):
                         scale = wsc[b][:, g, 512 * hq + P * c : 512 * hq + P * (c + 1)]
                         byte = 1024 * hq + 256 * c
                         nc.tensor.matmul_mx(
                             out=mx1[:, c, :],
-                            lhsT=wt[b][:, g, byte : byte + 256].bitcast(FP4X4),
+                            lhsT=(wt[b][:, g, byte : byte + 256] if b else w_first[h][:, g, 256 * c : 256 * (c + 1)]).bitcast(FP4X4),
                             lhsT_scale=scale,
                             rhs=xc[:, a, g, :].bitcast(FP8X4),
                             rhs_scale=xcs[:, a, g, :],
                             start=(g == 0),
                             stop=(g == G - 1),
                         )
-            quad, j = divmod(n - MX2_LAG, 4)
             us = []
-            if n >= MX2_LAG and quad < units // 4:
-                for st in (2 * j, 2 * j + 1):
-                    u_ps = psum.tile([P, 512], F32, name="u_ps", tag="u", bufs=2)
+            width = 2 if n < units else 3
+            while todo and len(us) < width and n >= sum(groups[todo[0][0]]) - 1 + 5:
+                j, sts = todo.pop(0)
+                extra = len(us) == 2
+                cols = P * groups[j][1]
+                u_ps = psum.tile([P, 512], F32, name="u_ps", tag="mx1" if extra else "u", bufs=2)
+                for k, st in enumerate(sts):
                     nc.tensor.matmul_mx(
-                        out=u_ps[:],
+                        out=u_ps[:, cols * k : cols * (k + 1)],
                         lhsT=kc[:, 512 * st : 512 * (st + 1)].bitcast(FP8X4),
                         lhsT_scale=ksc[:, P * st : P * (st + 1)],
-                        rhs=zc_of[quad][:].bitcast(FP8X4),
-                        rhs_scale=zs_of[quad][:],
+                        rhs=zc_of[j][:].bitcast(FP8X4),
+                        rhs_scale=zs_of[j][:],
                         start=True,
                         stop=True,
                     )
-                    us.append((st, u_ps))
+                us.append((j, sts, u_ps, extra))
 
             m = n - 2
             if 0 <= m < units:
                 a = m // H
-                t1 = t1_of[m]
-                rinv = rinv_of[m]
-                pp = work.tile([P, D], F32, name="pp", tag="pp")
-                qq = work.tile([P, D], F32, name="qq", tag="qq")
+                ww = work.tile([P, D // 2, 4], F32, name="ww", tag="ww")
                 nc.vector.scalar_tensor_tensor(
-                    out=pp[:], in0=t1[:], scalar=rinv[:], in1=cos_d[:, a, :, :].rearrange("p r e -> p (r e)"),
+                    out=ww[:].rearrange("p r j -> p (r j)").rearrange("p (d k) -> p d k", k=2),
+                    in0=t1_of[m][:].unsqueeze(2).to_broadcast([P, D, 2]), scalar=rinv_of[m][:],
+                    in1=tab[:, a, :, :].rearrange("p r j -> p (r j)").rearrange("p (d k) -> p d k", k=2),
                     op0=ALU.mult, op1=ALU.mult,
                 )
-                nc.vector.scalar_tensor_tensor(
-                    out=qq[:].rearrange("p (r e) -> p r e", e=2),
-                    in0=t1[:].rearrange("p (r e) -> p r e", e=2)[:, :, ::-1],
-                    scalar=rinv[:],
-                    in1=sin_s[:, a, :, :],
-                    op0=ALU.mult, op1=ALU.mult,
-                )
-
-            vs = []
-            for st, u_ps in us:
-                v = work.tile([P, 512], F32, name="v", tag="v", bufs=6)
-                qa, qb = divmod(quad, NQ)
-                nc.vector.scalar_tensor_tensor(
-                    out=v[:], in0=u_ps[:], scalar=nkb[:, st : st + 1],
-                    in1=alpha_t[:, qa, 4 * qb : 4 * qb + 4, :].rearrange("p h i -> p (h i)"),
-                    op0=ALU.max, op1=ALU.mult,
-                )
-                vs.append((quad, st, v))
-            v_of[n] = vs
-            if 0 <= m < units:
                 z = work.tile([P, D], BF16, name="z", tag="z", align_bytes=64)
-                nc.vector.tensor_tensor(
+                wv = ww[:].rearrange("i r j -> i (r j)").rearrange("i (p u s e) -> i s u p e", u=2, s=2, e=2)
+                nc.gpsimd.tensor_tensor(
                     out=z[:].rearrange("i (u p e) -> i u p e", u=2, e=2),
-                    in0=pp[:].rearrange("i (p u e) -> i u p e", u=2, e=2),
-                    in1=qq[:].rearrange("i (p u e) -> i u p e", u=2, e=2),
-                    op=ALU.add,
+                    in0=wv[:, 0], in1=wv[:, 1], op=ALU.add,
                 )
                 z_of[m] = z
+
+            while ready:
+                zq = ready.pop(0)
+                zc = work.tile([P, P * groups[zq][1]], U32, name="zc", tag="zc", bufs=3, align_bytes=64)
+                zs = work.tile([P, P * groups[zq][1]], U8, name="zs", tag="zs", bufs=3, align_bytes=64)
+                nc.vector.quantize_mx(
+                    out=zc[:].bitcast(FP8X4), scales=zs[:], in_=grp_of[zq][:].rearrange("p n k -> p (n k)")
+                )
+                zc_of[zq], zs_of[zq] = zc, zs
+
+            vs = []
+            for j, sts, u_ps, extra in us:
+                qa, h0 = divmod(groups[j][0], H)
+                size = groups[j][1]
+                gates = alpha_t[:, qa, h0 : h0 + size, :].rearrange("p h i -> p (h i)")
+                for k, st in enumerate(sts):
+                    cols = slice(P * size * k, P * size * (k + 1))
+                    v = work.tile([P, P * size], F32, name="v", tag="v", bufs=10)
+                    if extra:
+                        r1 = work.tile([P, P * size], F32, name="r1", tag="r1", bufs=2)
+                        r2 = work.tile([P, P * size], F32, name="r2", tag="r2", bufs=2)
+                        nc.scalar.activation(out=r1[:], in_=u_ps[:, cols], func=ACT.Relu, bias=pkb[:, st : st + 1])
+                        nc.scalar.activation(out=r2[:], in_=r1[:], func=ACT.Identity, bias=nkb[:, st : st + 1])
+                        nc.gpsimd.tensor_tensor(out=v[:], in0=r2[:], in1=gates, op=ALU.mult)
+                    else:
+                        nc.vector.scalar_tensor_tensor(
+                            out=v[:], in0=u_ps[:, cols], scalar=nkb[:, st : st + 1], in1=gates, op0=ALU.max, op1=ALU.mult,
+                        )
+                    if n < units and size == 4 and (0.5 == 1 or (0.5 == 0.5 and st % 2 == 0)):
+                        w = work.tile([P, 256], F32, name="w", tag="w", bufs=4)
+                        nc.gpsimd.tensor_tensor(out=w[:], in0=v[:, 0:256], in1=v[:, 256:512], op=ALU.add)
+                        vs.append((j, st, w, 2))
+                    else:
+                        vs.append((j, st, v, size))
+            v_of[n] = vs
 
             if n < units:
                 h = n % H
@@ -259,7 +298,7 @@ def tile_shared_key_index_scores_f7_kernel(
                     nc.scalar.activation(out=sq[:, c, :], in_=mx1[:, c, :], func=ACT.Square, bias=bcol[:, k : k + 1])
                 for c in range(4):
                     k = 4 * h + c
-                    if n < 8 and c >= 2:
+                    if n < 8 and c >= 4 - 4:
                         nc.vector.tensor_scalar(
                             out=yg[:, c, :], in0=mx1[:, c, :], scalar1=gcol[:, k : k + 1], scalar2=gbcol[:, k : k + 1],
                             op0=ALU.mult, op1=ALU.add,
@@ -271,37 +310,12 @@ def tile_shared_key_index_scores_f7_kernel(
                         )
                 yg_of[n], sq_of[n] = yg, sq
 
-            gates = []
-            if 1 <= n < 5:
-                ab = (1, n - 1)
-                gates.append((ab, spread_gates(*ab)))
-            for pq, st, v in v_of.get(n - 1, []):
-                qa, qb = divmod(pq, NQ)
-                half, sc = divmod(st, 4)
-                if qb == 0 and sc == 0:
-                    acc[half] = psum.tile([P, 512], F32, name=f"acc{half}", tag=f"acc{half}", bufs=1)
-                for hh in range(4):
-                    nc.tensor.matmul(
-                        acc[half][:, P * sc : P * (sc + 1)], lhsT=v[:, P * hh : P * (hh + 1)], rhs=ident[:],
-                        is_transpose=True,
-                        start=(qb == 0 and sc == 0 and hh == 0),
-                        stop=(qb == NQ - 1 and sc == 3 and hh == 3),
-                    )
-                if qb == NQ - 1 and sc == 3:
-                    o = work.tile([P, 512], F32, name="o", tag="o", bufs=2)
-                    nc.vector.scalar_tensor_tensor(
-                        out=o[:], in0=kb_all[:, 512 * half : 512 * (half + 1)], scalar=asum4[:, qa : qa + 1],
-                        in1=acc[half][:], op0=ALU.mult, op1=ALU.add,
-                    )
-                    nc.sync.dma_start(out=out[P * qa : P * (qa + 1), 512 * half : 512 * (half + 1)], in_=o[:])
+            spread = []
+            if n < 8:
+                spread.append((divmod(n, NQ), spread_gates(*divmod(n, NQ))))
             mt, mz = n - 1, n - 3
             if 0 <= mt < units or 0 <= mz < units:
                 misc = psum.tile([P, 4, P], F32, name="misc", tag="misc", bufs=1)
-            if 0 <= mt < units:
-                t1 = psum.tile([P, D], F32, name="t1", tag="t1", bufs=2)
-                for c in range(4):
-                    nc.tensor.transpose(t1[:, P * c : P * (c + 1)], yg_of[mt][:, c, :], ident[:])
-                t1_of[mt] = t1
             if 0 <= mz < units:
                 words = z_of[mz][:].bitcast(F32)
                 for u in range(2):
@@ -312,6 +326,32 @@ def tile_shared_key_index_scores_f7_kernel(
                         misc[:, 0, :], lhsT=sq_of[mt][:, c, :], rhs=ident[:], is_transpose=True,
                         start=(c == 0), stop=(c == 3),
                     )
+            for j, st, v, parts in v_of.get(n - 1, []):
+                qa, h0 = divmod(groups[j][0], H)
+                opens, closes = h0 == 0, h0 + groups[j][1] == H
+                half, sc = divmod(st, 4)
+                if opens and sc == 0:
+                    acc[half] = psum.tile([P, 512], F32, name=f"acc{half}", tag=f"acc{half}", bufs=1)
+                for hh in range(parts):
+                    nc.tensor.matmul(
+                        acc[half][:, P * sc : P * (sc + 1)], lhsT=v[:, P * hh : P * (hh + 1)], rhs=ident[:],
+                        is_transpose=True,
+                        start=(opens and sc == 0 and hh == 0),
+                        stop=(closes and sc == 3 and hh == parts - 1),
+                    )
+                if closes and sc == 3:
+                    o = work.tile([P, 512], F32, name="o", tag="o", bufs=2)
+                    nc.vector.scalar_tensor_tensor(
+                        out=o[:], in0=kb_all[:, 512 * half : 512 * (half + 1)], scalar=asum4[:, qa : qa + 1],
+                        in1=acc[half][:], op0=ALU.mult, op1=ALU.add,
+                    )
+                    nc.sync.dma_start(out=out[P * qa : P * (qa + 1), 512 * half : 512 * (half + 1)], in_=o[:])
+            if 0 <= mt < units:
+                t1 = psum.tile([P, D], F32, name="t1", tag=("t1", "acc0", "acc1")[n % 3] if n < 8 else "t1", bufs=1)
+                for c in range(4):
+                    nc.tensor.transpose(t1[:, P * c : P * (c + 1)], yg_of[mt][:, c, :], ident[:])
+                t1_of[mt] = t1
+            if 0 <= mt < units:
                 ss = work.tile([P, 1], F32, name="ss", tag="ss")
                 junk = work.tile([P, P], F32, name="junk", tag="junk", bufs=2)
                 nc.scalar.activation(out=junk[:], in_=misc[:, 0, :], func=ACT.Identity, accum_out=ss[:])
@@ -319,22 +359,21 @@ def tile_shared_key_index_scores_f7_kernel(
                 nc.scalar.activation(out=rinv[:], in_=ss[:], func=ACT.Abs_reciprocal_sqrt, scale=1.0 / D)
                 rinv_of[mt] = rinv
             if 0 <= mz < units:
-                zq, zi = divmod(mz, 4)
+                zq, zi = group_of[mz]
                 if zi == 0:
-                    grp = work.tile([P, 4, P * 4], BF16, name="grp", tag="grp", bufs=2, align_bytes=64)
+                    grp = work.tile([P, groups[zq][1], P * 4], BF16, name="grp", tag="grp", bufs=2, align_bytes=64)
                     grp_of[zq] = grp
                 nc.scalar.copy(
                     out=grp_of[zq][:, zi, :].bitcast(F32).rearrange("p (i u) -> p i u", u=2),
                     in_=misc[:, 1:3, :].rearrange("p u i -> p i u"),
                 )
-                if zi == 3:
-                    zc = work.tile([P, 512], U32, name="zc", tag="zc", bufs=2, align_bytes=64)
-                    zs = work.tile([P, 512], U8, name="zs", tag="zs", bufs=2, align_bytes=64)
-                    nc.vector.quantize_mx(
-                        out=zc[:].bitcast(FP8X4), scales=zs[:], in_=grp_of[zq][:].rearrange("p n k -> p (n k)")
-                    )
-                    zc_of[zq], zs_of[zq] = zc, zs
-            for (ga, gb), at_ps in gates:
+                if zi == groups[zq][1] - 1:
+                    ready.append(zq)
+            for (ga, gb), at_ps in spread:
                 nc.scalar.copy(out=alpha_t[:, ga, 4 * gb : 4 * gb + 4, :], in_=at_ps[:])
-            if n == 0:
+            if n == 1:
+                x_scaled(1)
+            if n == 3:
                 x_quantized(1, x_turned(1))
+            n += 1
+            busy = bool(todo) or bool(vs)

@@ -119,11 +119,9 @@ def tile_shared_key_index_scores_f7_kernel(
         bcol = keep.tile([P, 64], F32, name="bcol")
         gbcol = keep.tile([P, 64], F32, name="gbcol")
         nkb = keep.tile([P, 8], F32, name="nkb")
-        pkb = keep.tile([P, 8], F32, name="pkb")
         nc.vector.tensor_copy(out=gcol[:], in_=cols_ps[:, 0, 0:64])
         nc.vector.tensor_copy(out=bcol[:], in_=cols_ps[:, 0, 64:128])
         nc.vector.tensor_scalar(out=nkb[:], in0=cols_ps[:, 1, 0:8], scalar1=-ROOT_D, scalar2=None, op0=ALU.mult)
-        nc.vector.tensor_scalar(out=pkb[:], in0=cols_ps[:, 1, 0:8], scalar1=ROOT_D, scalar2=None, op0=ALU.mult)
         nc.vector.tensor_tensor(out=gbcol[:], in0=gcol[:], in1=bcol[:], op=ALU.mult)
         xp = keep.tile([P, NA, G, 512], BF16, name="xp", align_bytes=64)
         xc = keep.tile([P, NA, G, P], U32, name="xc", align_bytes=64)
@@ -184,196 +182,243 @@ def tile_shared_key_index_scores_f7_kernel(
                 nc.gpsimd.tensor_scalar(out=tab[:, a, :, j], in0=src[:, a, :], scalar1=sign, scalar2=0.0, op0=ALU.mult, op1=ALU.add)
 
         units = NA * H
-        yg_of, sq_of, t1_of, rinv_of, z_of = {}, {}, {}, {}, {}
-        grp_of, zc_of, zs_of, v_of = {}, {}, {}, {}
+        quads = units // 4
+        yg_of, sq_of, t1_of, rinv_of, z_of, misc_of, grp_of, zc_of, zs_of = {}, {}, {}, {}, {}, {}, {}, {}, {}
         acc = {}
-        ready = []
-        groups = []
-        for size in [4] * 8:
-            first = groups[-1][0] + groups[-1][1] if groups else 0
-            groups.append((first, size))
-        group_of = {first + k: (j, k) for j, (first, size) in enumerate(groups) for k in range(size)}
-        todo = []
-        for j, (first, size) in enumerate(groups):
-            step = 4 // size
-            todo.extend((j, range(st, st + step)) for st in range(0, 8, step))
-        n = 0
-        busy = True
-        while busy:
-            if n < units:
-                a, h = divmod(n, H)
-                b, hq = divmod(h, 4)
-                mx1 = psum.tile([P, 4, P], F32, name="mx1", tag="mx1", bufs=2)
-                for c in range(4):
-                    for g in range(G):
-                        scale = wsc[b][:, g, 512 * hq + P * c : 512 * hq + P * (c + 1)]
-                        byte = 1024 * hq + 256 * c
-                        nc.tensor.matmul_mx(
-                            out=mx1[:, c, :],
-                            lhsT=(wt[b][:, g, byte : byte + 256] if b else w_first[h][:, g, 256 * c : 256 * (c + 1)]).bitcast(FP4X4),
-                            lhsT_scale=scale,
-                            rhs=xc[:, a, g, :].bitcast(FP8X4),
-                            rhs_scale=xcs[:, a, g, :],
-                            start=(g == 0),
-                            stop=(g == G - 1),
-                        )
-            us = []
-            width = 2 if n < units else 3
-            while todo and len(us) < width and n >= sum(groups[todo[0][0]]) - 1 + 5:
-                j, sts = todo.pop(0)
-                extra = len(us) == 2
-                cols = P * groups[j][1]
-                u_ps = psum.tile([P, 512], F32, name="u_ps", tag="mx1" if extra else "u", bufs=2)
-                for k, st in enumerate(sts):
+
+        def first_matmul(n):
+            a, h = divmod(n, H)
+            b, hq = divmod(h, 4)
+            mx1 = psum.tile([P, 4, P], F32, name="mx1", tag="mx1", bufs=2)
+            for c in range(4):
+                for g in range(G):
+                    if b == 0:
+                        words = w_first[h][:, g, 256 * c : 256 * (c + 1)]
+                    else:
+                        words = wt[b][:, g, 1024 * hq + 256 * c : 1024 * hq + 256 * (c + 1)]
                     nc.tensor.matmul_mx(
-                        out=u_ps[:, cols * k : cols * (k + 1)],
-                        lhsT=kc[:, 512 * st : 512 * (st + 1)].bitcast(FP8X4),
-                        lhsT_scale=ksc[:, P * st : P * (st + 1)],
-                        rhs=zc_of[j][:].bitcast(FP8X4),
-                        rhs_scale=zs_of[j][:],
-                        start=True,
-                        stop=True,
+                        out=mx1[:, c, :],
+                        lhsT=words.bitcast(FP4X4),
+                        lhsT_scale=wsc[b][:, g, 512 * hq + P * c : 512 * hq + P * (c + 1)],
+                        rhs=xc[:, a, g, :].bitcast(FP8X4),
+                        rhs_scale=xcs[:, a, g, :],
+                        start=(g == 0),
+                        stop=(g == G - 1),
                     )
-                us.append((j, sts, u_ps, extra))
+            return mx1
 
-            m = n - 2
-            if 0 <= m < units:
-                a = m // H
-                ww = work.tile([P, D // 2, 4], F32, name="ww", tag="ww")
+        def leave_first(n, mx1):
+            h = n % H
+            yg = work.tile([P, 4, P], F32, name="yg", tag="yg")
+            sq = work.tile([P, 4, P], F32, name="sq", tag="sq")
+            for c in range(4):
+                k = 4 * h + c
+                nc.scalar.activation(out=sq[:, c, :], in_=mx1[:, c, :], func=ACT.Square, bias=bcol[:, k : k + 1])
+            for c in range(4):
+                k = 4 * h + c
+                if n < 9 and c >= 4 - 4:
+                    nc.vector.tensor_scalar(
+                        out=yg[:, c, :], in0=mx1[:, c, :], scalar1=gcol[:, k : k + 1], scalar2=gbcol[:, k : k + 1],
+                        op0=ALU.mult, op1=ALU.add,
+                    )
+                else:
+                    nc.scalar.activation(
+                        out=yg[:, c, :], in_=mx1[:, c, :], func=ACT.Identity,
+                        bias=gbcol[:, k : k + 1], scale=gcol[:, k : k + 1],
+                    )
+            yg_of[n], sq_of[n] = yg, sq
+
+        def turn_y(n, bank):
+            t1 = psum.tile([P, D], F32, name="t1", tag=bank, bufs=2 if bank == "mx1" else 1)
+            for c in range(4):
+                nc.tensor.transpose(t1[:, P * c : P * (c + 1)], yg_of[n][:, c, :], ident[:])
+            t1_of[n] = t1
+
+        def add_squares(n, misc):
+            for c in range(4):
+                nc.tensor.matmul(
+                    misc[:, 0, :], lhsT=sq_of[n][:, c, :], rhs=ident[:], is_transpose=True,
+                    start=(c == 0), stop=(c == 3),
+                )
+
+        def inverse_rms(n, misc):
+            ss = work.tile([P, 1], F32, name="ss", tag="ss")
+            junk = work.tile([P, P], F32, name="junk", tag="junk", bufs=2)
+            nc.scalar.activation(out=junk[:], in_=misc[:, 0, :], func=ACT.Identity, accum_out=ss[:])
+            rinv = work.tile([P, 1], F32, name="rinv", tag="rinv", bufs=4)
+            nc.scalar.activation(out=rinv[:], in_=ss[:], func=ACT.Abs_reciprocal_sqrt, scale=1.0 / D)
+            rinv_of[n] = rinv
+
+        def rotate(n, on_vector):
+            ww = work.tile([P, D // 2, 4], F32, name="ww", tag="ww")
+            nc.vector.scalar_tensor_tensor(
+                out=ww[:].rearrange("p r j -> p (r j)").rearrange("p (d k) -> p d k", k=2),
+                in0=t1_of[n][:].unsqueeze(2).to_broadcast([P, D, 2]), scalar=rinv_of[n][:],
+                in1=tab[:, n // H, :, :].rearrange("p r j -> p (r j)").rearrange("p (d k) -> p d k", k=2),
+                op0=ALU.mult, op1=ALU.mult,
+            )
+            z = work.tile([P, D], BF16, name="z", tag="z", bufs=4, align_bytes=64)
+            wv = ww[:].rearrange("i r j -> i (r j)").rearrange("i (p u s e) -> i s u p e", u=2, s=2, e=2)
+            engine = nc.vector if on_vector else nc.gpsimd
+            engine.tensor_tensor(
+                out=z[:].rearrange("i (u p e) -> i u p e", u=2, e=2), in0=wv[:, 0], in1=wv[:, 1], op=ALU.add,
+            )
+            z_of[n] = z
+
+        def turn_z(n, misc):
+            words = z_of[n][:].bitcast(F32)
+            for u in range(2):
+                nc.tensor.transpose(misc[:, 1 + u, :], words[:, P * u : P * (u + 1)], ident[:])
+
+        def leave_z(n, misc):
+            q, k = divmod(n, 4)
+            if k == 0:
+                grp = work.tile([P, 4, P * 4], BF16, name="grp", tag="grp", bufs=2, align_bytes=64)
+                grp_of[q] = grp
+            nc.scalar.copy(
+                out=grp_of[q][:, k, :].bitcast(F32).rearrange("p (i u) -> p i u", u=2),
+                in_=misc[:, 1:3, :].rearrange("p u i -> p i u"),
+            )
+
+        def quantize(q):
+            zc = work.tile([P, 512], U32, name="zc", tag="zc", bufs=2, align_bytes=64)
+            zs = work.tile([P, 512], U8, name="zs", tag="zs", bufs=2, align_bytes=64)
+            nc.vector.quantize_mx(out=zc[:].bitcast(FP8X4), scales=zs[:], in_=grp_of[q][:].rearrange("p n k -> p (n k)"))
+            zc_of[q], zs_of[q] = zc, zs
+
+        def second_matmul(q, st, extra):
+            u_ps = psum.tile([P, 512], F32, name="u_ps", tag="mx1" if extra else "u", bufs=2)
+            nc.tensor.matmul_mx(
+                out=u_ps[:],
+                lhsT=kc[:, 512 * st : 512 * (st + 1)].bitcast(FP8X4),
+                lhsT_scale=ksc[:, P * st : P * (st + 1)],
+                rhs=zc_of[q][:].bitcast(FP8X4),
+                rhs_scale=zs_of[q][:],
+                start=True,
+                stop=True,
+            )
+            return u_ps
+
+        def gate(q, st, u_ps, pair):
+            a, b = divmod(q, NQ)
+            gates = alpha_t[:, a, 4 * b : 4 * b + 4, :].rearrange("p h i -> p (h i)")
+            v = work.tile([P, 512], F32, name="v", tag="v", bufs=10)
+            nc.vector.scalar_tensor_tensor(
+                out=v[:], in0=u_ps[:], scalar=nkb[:, st : st + 1], in1=gates, op0=ALU.max, op1=ALU.mult,
+            )
+            if pair:
+                w = work.tile([P, 256], F32, name="w", tag="w", bufs=6)
+                nc.gpsimd.tensor_tensor(out=w[:], in0=v[:, 0:256], in1=v[:, 256:512], op=ALU.add)
+                return w, 2
+            return v, 4
+
+        count = {}
+
+        def pool_heads(q, st, v, parts):
+            a, b = divmod(q, NQ)
+            half, sc = divmod(st, 4)
+            done = count.get((a, half), 0)
+            if done == 0:
+                acc[half] = psum.tile([P, 512], F32, name=f"acc{half}", tag=f"acc{half}", bufs=1)
+            last = done == 4 * NQ - 1
+            for hh in range(parts):
+                nc.tensor.matmul(
+                    acc[half][:, P * sc : P * (sc + 1)], lhsT=v[:, P * hh : P * (hh + 1)], rhs=ident[:],
+                    is_transpose=True,
+                    start=(done == 0 and hh == 0),
+                    stop=(last and hh == parts - 1),
+                )
+            count[(a, half)] = done + 1
+            if last:
+                o = work.tile([P, 512], F32, name="o", tag="o", bufs=2)
                 nc.vector.scalar_tensor_tensor(
-                    out=ww[:].rearrange("p r j -> p (r j)").rearrange("p (d k) -> p d k", k=2),
-                    in0=t1_of[m][:].unsqueeze(2).to_broadcast([P, D, 2]), scalar=rinv_of[m][:],
-                    in1=tab[:, a, :, :].rearrange("p r j -> p (r j)").rearrange("p (d k) -> p d k", k=2),
-                    op0=ALU.mult, op1=ALU.mult,
+                    out=o[:], in0=kb_all[:, 512 * half : 512 * (half + 1)], scalar=asum4[:, a : a + 1],
+                    in1=acc[half][:], op0=ALU.mult, op1=ALU.add,
                 )
-                z = work.tile([P, D], BF16, name="z", tag="z", align_bytes=64)
-                wv = ww[:].rearrange("i r j -> i (r j)").rearrange("i (p u s e) -> i s u p e", u=2, s=2, e=2)
-                nc.gpsimd.tensor_tensor(
-                    out=z[:].rearrange("i (u p e) -> i u p e", u=2, e=2),
-                    in0=wv[:, 0], in1=wv[:, 1], op=ALU.add,
-                )
-                z_of[m] = z
+                nc.sync.dma_start(out=out[P * a : P * (a + 1), 512 * half : 512 * (half + 1)], in_=o[:])
 
-            while ready:
-                zq = ready.pop(0)
-                zc = work.tile([P, P * groups[zq][1]], U32, name="zc", tag="zc", bufs=3, align_bytes=64)
-                zs = work.tile([P, P * groups[zq][1]], U8, name="zs", tag="zs", bufs=3, align_bytes=64)
-                nc.vector.quantize_mx(
-                    out=zc[:].bitcast(FP8X4), scales=zs[:], in_=grp_of[zq][:].rearrange("p n k -> p (n k)")
-                )
-                zc_of[zq], zs_of[zq] = zc, zs
-
-            vs = []
-            for j, sts, u_ps, extra in us:
-                qa, h0 = divmod(groups[j][0], H)
-                size = groups[j][1]
-                gates = alpha_t[:, qa, h0 : h0 + size, :].rearrange("p h i -> p (h i)")
-                for k, st in enumerate(sts):
-                    cols = slice(P * size * k, P * size * (k + 1))
-                    v = work.tile([P, P * size], F32, name="v", tag="v", bufs=10)
-                    if extra:
-                        r1 = work.tile([P, P * size], F32, name="r1", tag="r1", bufs=2)
-                        r2 = work.tile([P, P * size], F32, name="r2", tag="r2", bufs=2)
-                        nc.scalar.activation(out=r1[:], in_=u_ps[:, cols], func=ACT.Relu, bias=pkb[:, st : st + 1])
-                        nc.scalar.activation(out=r2[:], in_=r1[:], func=ACT.Identity, bias=nkb[:, st : st + 1])
-                        nc.gpsimd.tensor_tensor(out=v[:], in0=r2[:], in1=gates, op=ALU.mult)
-                    else:
-                        nc.vector.scalar_tensor_tensor(
-                            out=v[:], in0=u_ps[:, cols], scalar=nkb[:, st : st + 1], in1=gates, op0=ALU.max, op1=ALU.mult,
-                        )
-                    if n < units and size == 4 and (0.5 == 1 or (0.5 == 0.5 and st % 2 == 0)):
-                        w = work.tile([P, 256], F32, name="w", tag="w", bufs=4)
-                        nc.gpsimd.tensor_tensor(out=w[:], in0=v[:, 0:256], in1=v[:, 256:512], op=ALU.add)
-                        vs.append((j, st, w, 2))
-                    else:
-                        vs.append((j, st, v, size))
-            v_of[n] = vs
-
-            if n < units:
-                h = n % H
-                yg = work.tile([P, 4, P], F32, name="yg", tag="yg")
-                sq = work.tile([P, 4, P], F32, name="sq", tag="sq")
-                for c in range(4):
-                    k = 4 * h + c
-                    nc.scalar.activation(out=sq[:, c, :], in_=mx1[:, c, :], func=ACT.Square, bias=bcol[:, k : k + 1])
-                for c in range(4):
-                    k = 4 * h + c
-                    if n < 8 and c >= 4 - 4:
-                        nc.vector.tensor_scalar(
-                            out=yg[:, c, :], in0=mx1[:, c, :], scalar1=gcol[:, k : k + 1], scalar2=gbcol[:, k : k + 1],
-                            op0=ALU.mult, op1=ALU.add,
-                        )
-                    else:
-                        nc.scalar.activation(
-                            out=yg[:, c, :], in_=mx1[:, c, :], func=ACT.Identity,
-                            bias=gbcol[:, k : k + 1], scale=gcol[:, k : k + 1],
-                        )
-                yg_of[n], sq_of[n] = yg, sq
-
-            spread = []
-            if n < 8:
-                spread.append((divmod(n, NQ), spread_gates(*divmod(n, NQ))))
-            mt, mz = n - 1, n - 3
-            if 0 <= mt < units or 0 <= mz < units:
+        todo = [(q, st) for q in range(quads) for st in range(8)]
+        rest = []
+        ZL = 4
+        WL = 2
+        n = 0
+        while n < units or todo or rest:
+            steady = n < units
+            if steady:
+                mx1 = first_matmul(n)
+            width = 2 if steady else 4
+            items = []
+            def scores():
+                while todo and len(items) < width and todo[0][0] in zc_of and (not steady or n >= 4 * todo[0][0] + 5 + ZL):
+                    q, st = todo.pop(0)
+                    extra = len(items) >= 2
+                    items.append((q, st, second_matmul(q, st, extra)))
+            def gated():
+                for q, st, u_ps in items:
+                    pair = steady and (st % 2 == 0)
+                    v, parts = gate(q, st, u_ps, pair)
+                    rest.append((n + (WL if pair else 1), q, st, v, parts))
+            def pooled():
+                for item in [r for r in rest if r[0] <= n]:
+                    rest.remove(item)
+                    pool_heads(*item[1:])
+            if steady:
+                scores()
+                if 0 <= n - 2:
+                    rotate(n - 2, False)
+                if n - ZL - 1 >= 0 and (n - ZL - 1) % 4 == 3:
+                    quantize((n - ZL - 1) // 4)
+                gated()
+                leave_first(n, mx1)
+                if n < 8:
+                    a, b = divmod(n, NQ)
+                    at_ps = spread_gates(a, b)
+                if n >= 1:
+                    misc = psum.tile([P, 4, P], F32, name="misc", tag="misc", bufs=1)
+                    if n >= ZL:
+                        turn_z(n - ZL, misc)
+                    add_squares(n - 1, misc)
+                pooled()
+                if n >= 1:
+                    turn_y(n - 1, ("t1", "acc0", "acc1")[n % 3] if n < 8 else "t1")
+                    inverse_rms(n - 1, misc)
+                if n >= ZL:
+                    leave_z(n - ZL, misc)
+                if n < 8:
+                    nc.scalar.copy(out=alpha_t[:, a, 4 * b : 4 * b + 4, :], in_=at_ps[:])
+                if n == 1:
+                    x_scaled(1)
+                if n == 3:
+                    x_quantized(1, x_turned(1))
+            elif n == units:
+                scores()
+                misc = psum.tile([P, 4, P], F32, name="misc", tag="mx1", bufs=2)
+                add_squares(n - 1, misc)
+                turn_z(n - ZL, misc)
+                rotate(n - 2, False)
+                quantize(quads - 2)
+                gated()
+                inverse_rms(n - 1, misc)
+                leave_z(n - ZL, misc)
+                turn_y(n - 1, "mx1")
+                rotate(n - 1, True)
+                pooled()
+            elif n == units + 1:
+                scores()
                 misc = psum.tile([P, 4, P], F32, name="misc", tag="misc", bufs=1)
-            if 0 <= mz < units:
-                words = z_of[mz][:].bitcast(F32)
-                for u in range(2):
-                    nc.tensor.transpose(misc[:, 1 + u, :], words[:, P * u : P * (u + 1)], ident[:])
-            if 0 <= mt < units:
-                for c in range(4):
-                    nc.tensor.matmul(
-                        misc[:, 0, :], lhsT=sq_of[mt][:, c, :], rhs=ident[:], is_transpose=True,
-                        start=(c == 0), stop=(c == 3),
-                    )
-            for j, st, v, parts in v_of.get(n - 1, []):
-                qa, h0 = divmod(groups[j][0], H)
-                opens, closes = h0 == 0, h0 + groups[j][1] == H
-                half, sc = divmod(st, 4)
-                if opens and sc == 0:
-                    acc[half] = psum.tile([P, 512], F32, name=f"acc{half}", tag=f"acc{half}", bufs=1)
-                for hh in range(parts):
-                    nc.tensor.matmul(
-                        acc[half][:, P * sc : P * (sc + 1)], lhsT=v[:, P * hh : P * (hh + 1)], rhs=ident[:],
-                        is_transpose=True,
-                        start=(opens and sc == 0 and hh == 0),
-                        stop=(closes and sc == 3 and hh == parts - 1),
-                    )
-                if closes and sc == 3:
-                    o = work.tile([P, 512], F32, name="o", tag="o", bufs=2)
-                    nc.vector.scalar_tensor_tensor(
-                        out=o[:], in0=kb_all[:, 512 * half : 512 * (half + 1)], scalar=asum4[:, qa : qa + 1],
-                        in1=acc[half][:], op0=ALU.mult, op1=ALU.add,
-                    )
-                    nc.sync.dma_start(out=out[P * qa : P * (qa + 1), 512 * half : 512 * (half + 1)], in_=o[:])
-            if 0 <= mt < units:
-                t1 = psum.tile([P, D], F32, name="t1", tag=("t1", "acc0", "acc1")[n % 3] if n < 8 else "t1", bufs=1)
-                for c in range(4):
-                    nc.tensor.transpose(t1[:, P * c : P * (c + 1)], yg_of[mt][:, c, :], ident[:])
-                t1_of[mt] = t1
-            if 0 <= mt < units:
-                ss = work.tile([P, 1], F32, name="ss", tag="ss")
-                junk = work.tile([P, P], F32, name="junk", tag="junk", bufs=2)
-                nc.scalar.activation(out=junk[:], in_=misc[:, 0, :], func=ACT.Identity, accum_out=ss[:])
-                rinv = work.tile([P, 1], F32, name="rinv", tag="rinv", bufs=4)
-                nc.scalar.activation(out=rinv[:], in_=ss[:], func=ACT.Abs_reciprocal_sqrt, scale=1.0 / D)
-                rinv_of[mt] = rinv
-            if 0 <= mz < units:
-                zq, zi = group_of[mz]
-                if zi == 0:
-                    grp = work.tile([P, groups[zq][1], P * 4], BF16, name="grp", tag="grp", bufs=2, align_bytes=64)
-                    grp_of[zq] = grp
-                nc.scalar.copy(
-                    out=grp_of[zq][:, zi, :].bitcast(F32).rearrange("p (i u) -> p i u", u=2),
-                    in_=misc[:, 1:3, :].rearrange("p u i -> p i u"),
-                )
-                if zi == groups[zq][1] - 1:
-                    ready.append(zq)
-            for (ga, gb), at_ps in spread:
-                nc.scalar.copy(out=alpha_t[:, ga, 4 * gb : 4 * gb + 4, :], in_=at_ps[:])
-            if n == 1:
-                x_scaled(1)
-            if n == 3:
-                x_quantized(1, x_turned(1))
+                late = psum.tile([P, 4, P], F32, name="late", tag="t1", bufs=1)
+                turn_z(units - 3, misc)
+                leave_z(units - 3, misc)
+                turn_z(units - 2, late)
+                leave_z(units - 2, late)
+                pooled()
+                last = psum.tile([P, 4, P], F32, name="last", tag="misc", bufs=1)
+                turn_z(units - 1, last)
+                leave_z(units - 1, last)
+                gated()
+                quantize(quads - 1)
+            else:
+                scores()
+                gated()
+                pooled()
             n += 1
-            busy = bool(todo) or bool(vs)

import math
from contextlib import ExitStack

import concourse.mybir as mybir
from concourse.masks import make_identity

T, E, H, D, S = 256, 1024, 16, 512, 1024
FLOPS = 2 * T * E * H * D + 2 * T * H * D * S

F32 = mybir.dt.float32
BF16 = mybir.dt.bfloat16
I32 = mybir.dt.int32
U32 = mybir.dt.uint32
U8 = mybir.dt.uint8
FP8 = mybir.dt.float8_e4m3fn
FP8X4 = mybir.dt.float8_e4m3fn_x4
FP4X4 = mybir.dt.float4_e2m1fn_x4
ALU = mybir.AluOpType
ACT = mybir.ActivationFunctionType

P = 128
G = E // 512
NA = T // P
NQ = 4
ROOT_D = math.sqrt(D)


def tile_shared_key_index_scores_f7_kernel(
    tc, x_bytes, x_scale, wq_words, wq_scales, bias, gain, cosines, sines,
    k_words, k_scales, key_bias, head_gate, out,
):
    nc = tc.nc
    with ExitStack() as ctx:
        keep = ctx.enter_context(tc.tile_pool(name="keep", bufs=1))
        work = ctx.enter_context(tc.tile_pool(name="work", bufs=3))
        psum = ctx.enter_context(tc.psum_pool(name="psum", bufs=1))
        ctx.enter_context(tc.manual_schedule())

        gb_rows = keep.tile([P, P], BF16, name="gb_rows")
        nc.scalar.dma_start(out=gb_rows[0:64, :], in_=gain.rearrange("h (c m) -> (h c) m", m=P))
        nc.scalar.dma_start(out=gb_rows[64:128, :], in_=bias.rearrange("(c m) -> c m", m=P))
        hg = keep.tile([P, NA, H], BF16, name="hg")
        nc.scalar.dma_start(out=hg[:], in_=head_gate.rearrange("(a p) h -> p a h", p=P))

        xb = []
        for a in range(NA):
            x_raw = keep.tile([P, E], U8, name=f"xb{a}", align_bytes=64)
            xb.append(x_raw)
        xs = []
        for g in range(G):
            xs_half = keep.tile([P, 512], F32, name=f"xs{g}")
            xs.append(xs_half)
        nc.sync.dma_start(out=xb[0][:], in_=x_bytes[0:P, :])
        for g in range(G):
            nc.sync.dma_start(out=xs[g][:], in_=x_scale[0, 512 * g : 512 * (g + 1)].partition_broadcast(P))

        wsc = []
        for b in range(NQ):
            ws = keep.tile([P, G, 2048], U8, name=f"wsc{b}", align_bytes=64)
            wsc.append(ws)
        ksc = keep.tile([P, S], U8, name="ksc", align_bytes=64)
        kb_rows = keep.tile([P, P], BF16, name="kb_rows")
        nc.vector.memset(wsc[0][:].rearrange("p g n -> p (g n)").bitcast(I32), 0)
        nc.vector.memset(kb_rows[:], 0.0)
        nc.vector.memset(wsc[1][:].rearrange("p g n -> p (g n)").bitcast(I32), 0)
        nc.vector.memset(ksc[:].bitcast(I32), 0)
        nc.vector.memset(wsc[2][:].rearrange("p g n -> p (g n)").bitcast(I32), 0)
        nc.vector.memset(wsc[3][:].rearrange("p g n -> p (g n)").bitcast(I32), 0)
        nc.scalar.dma_start(out=kb_rows[0:8, :], in_=key_bias.rearrange("(c m) -> c m", m=P))

        wt = [None]
        for b in range(1, NQ):
            w = keep.tile([P, G, 4096], U8, name=f"w{b}", align_bytes=64)
            wt.append(w)
        w_first = []
        for h in range(4):
            w = keep.tile([P, G, 1024], U8, name=f"wf{h}", align_bytes=64)
            w_first.append(w)
        cs = keep.tile([P, NA, D // 2], BF16, name="cs")
        sn = keep.tile([P, NA, D // 2], BF16, name="sn")
        kc = keep.tile([P, 4 * S], U8, name="kc", align_bytes=64)
        kb_all = keep.tile([P, S], BF16, name="kb_all")

        def load_weights(b):
            for q in range(4):
                nc.sync.dma_start(
                    out=wsc[b][32 * q : 32 * q + 4, :, :].bitcast(I32),
                    in_=wq_scales[:, 4 * q : 4 * q + 4, 2048 * b : 2048 * (b + 1)].rearrange("g r n -> r g n").bitcast(I32),
                )
            for h in range(4 * b, 4 * b + 4) if b == 0 else ():
                nc.sync.dma_start(out=w_first[h][:], in_=wq_words[:, :, 1024 * h : 1024 * (h + 1)].rearrange("g p n -> p g n"))
            if b:
                nc.sync.dma_start(out=wt[b][:], in_=wq_words[:, :, 4096 * b : 4096 * (b + 1)].rearrange("g p n -> p g n"))

        load_weights(0)
        nc.sync.dma_start(out=cs[:], in_=cosines.rearrange("(a p) r -> p a r", p=P))
        nc.sync.dma_start(out=sn[:], in_=sines.rearrange("(a p) r -> p a r", p=P))
        nc.sync.dma_start(out=xb[1][:], in_=x_bytes[P : 2 * P, :])
        load_weights(1)
        for q in range(4):
            nc.sync.dma_start(
                out=ksc[32 * q : 32 * q + 4, :].bitcast(I32),
                in_=k_scales[0, 4 * q : 4 * q + 4, :].bitcast(I32),
            )
        nc.sync.dma_start(out=kc[:], in_=k_words[0].rearrange("p n t -> p (n t)"))
        load_weights(2)
        load_weights(3)
        nc.sync.dma_start(out=kb_all[:], in_=key_bias.partition_broadcast(P))

        ident = keep.tile([P, P], F32, name="ident")
        make_identity(nc, ident[:])
        identb = keep.tile([P, P], BF16, name="identb")
        make_identity(nc, identb[:])

        cols_ps = psum.tile([P, 2, P], BF16, name="cols_ps", tag="u", bufs=2)
        nc.tensor.transpose(cols_ps[:, 0, :], gb_rows[:], identb[:])
        nc.tensor.transpose(cols_ps[:, 1, :], kb_rows[:], identb[:])
        gcol = keep.tile([P, 64], F32, name="gcol")
        bcol = keep.tile([P, 64], F32, name="bcol")
        gbcol = keep.tile([P, 64], F32, name="gbcol")
        nkb = keep.tile([P, 8], F32, name="nkb")
        nc.vector.tensor_copy(out=gcol[:], in_=cols_ps[:, 0, 0:64])
        nc.vector.tensor_copy(out=bcol[:], in_=cols_ps[:, 0, 64:128])
        nc.vector.tensor_scalar(out=nkb[:], in0=cols_ps[:, 1, 0:8], scalar1=-ROOT_D, scalar2=None, op0=ALU.mult)
        nc.vector.tensor_tensor(out=gbcol[:], in0=gcol[:], in1=bcol[:], op=ALU.mult)
        xp = keep.tile([P, NA, G, 512], BF16, name="xp", align_bytes=64)
        xc = keep.tile([P, NA, G, P], U32, name="xc", align_bytes=64)
        xcs = keep.tile([P, NA, G, P], U8, name="xcs", align_bytes=64)
        xg = keep.tile([P, NA, G, P * 4], BF16, name="xg", align_bytes=64)

        def x_scaled(a):
            for g in range(G):
                nc.vector.tensor_tensor(out=xp[:, a, g, :], in0=xb[a][:, 512 * g : 512 * (g + 1)].bitcast(FP8), in1=xs[g][:], op=ALU.mult)

        def x_turned(a):
            turned = []
            for g in range(G):
                words = xp[:, a, g, :].bitcast(F32)
                xt_ps = psum.tile([P, 2, P], F32, name="xt_ps", tag=f"acc{g}", bufs=1)
                for u in range(2):
                    nc.tensor.transpose(xt_ps[:, u, :], words[:, u::2], ident[:])
                turned.append(xt_ps)
            return turned

        def x_quantized(a, turned):
            for g in range(G):
                nc.vector.tensor_copy(
                    out=xg[:, a, g, :].bitcast(F32).rearrange("p (i u) -> p i u", u=2),
                    in_=turned[g][:].rearrange("p u i -> p i u"),
                )
            nc.vector.quantize_mx(
                out=xc[:, a, :, :].rearrange("p g i -> p (g i)").bitcast(FP8X4),
                scales=xcs[:, a, :, :].rearrange("p g i -> p (g i)"), in_=xg[:, a, :, :].rearrange("p g k -> p (g k)"),
            )

        x_scaled(0)
        xt0 = x_turned(0)
        x_quantized(0, xt0)

        alpha = keep.tile([P, NA, H], F32, name="alpha")
        asum = keep.tile([P, NA], F32, name="asum")
        for a in range(NA):
            nc.scalar.activation(out=alpha[:, a, :], in_=hg[:, a, :], func=ACT.Sigmoid, accum_out=asum[:, a : a + 1])
        warm = keep.tile([P, 1], F32, name="warm")
        nc.scalar.activation(out=warm[:], in_=asum[:, 0:1], func=ACT.Abs_reciprocal_sqrt)
        alpha_s = keep.tile([P, NA, H], F32, name="alpha_s")
        nc.vector.tensor_scalar(out=alpha_s[:], in0=alpha[:], scalar1=1.0 / (4.0 * ROOT_D), scalar2=None, op0=ALU.mult)
        asum4 = keep.tile([P, NA], F32, name="asum4")
        nc.vector.tensor_scalar(out=asum4[:], in0=asum[:], scalar1=0.25, scalar2=None, op0=ALU.mult)
        alpha_t = keep.tile([P, NA, H, P], F32, name="alpha_t")

        def spread_gates(a, b):
            at_ps = psum.tile([P, 4, P], F32, name="at_ps", tag="u", bufs=2)
            for hh in range(4):
                h = 4 * b + hh
                nc.tensor.transpose(at_ps[:, hh, :], alpha_s[:, a, h : h + 1].to_broadcast([P, P]), ident[:])
            return at_ps

        tab = keep.tile([P, NA, D // 2, 4], BF16, name="tab")
        for a in range(NA):
            for j, (src, sign) in enumerate(((cs, 1.0), (sn, 1.0), (sn, -1.0), (cs, 1.0))):
                nc.gpsimd.tensor_scalar(out=tab[:, a, :, j], in0=src[:, a, :], scalar1=sign, scalar2=0.0, op0=ALU.mult, op1=ALU.add)

        units = NA * H
        quads = units // 4
        yg_of, sq_of, t1_of, rinv_of, z_of, misc_of, grp_of, zc_of, zs_of = {}, {}, {}, {}, {}, {}, {}, {}, {}
        acc = {}

        def first_matmul(n):
            a, h = divmod(n, H)
            b, hq = divmod(h, 4)
            mx1 = psum.tile([P, 4, P], F32, name="mx1", tag="mx1", bufs=2)
            for c in range(4):
                for g in range(G):
                    if b == 0:
                        words = w_first[h][:, g, 256 * c : 256 * (c + 1)]
                    else:
                        words = wt[b][:, g, 1024 * hq + 256 * c : 1024 * hq + 256 * (c + 1)]
                    nc.tensor.matmul_mx(
                        out=mx1[:, c, :],
                        lhsT=words.bitcast(FP4X4),
                        lhsT_scale=wsc[b][:, g, 512 * hq + P * c : 512 * hq + P * (c + 1)],
                        rhs=xc[:, a, g, :].bitcast(FP8X4),
                        rhs_scale=xcs[:, a, g, :],
                        start=(g == 0),
                        stop=(g == G - 1),
                    )
            return mx1

        def leave_first(n, mx1):
            h = n % H
            yg = work.tile([P, 4, P], F32, name="yg", tag="yg")
            sq = work.tile([P, 4, P], F32, name="sq", tag="sq")
            for c in range(4):
                k = 4 * h + c
                nc.scalar.activation(out=sq[:, c, :], in_=mx1[:, c, :], func=ACT.Square, bias=bcol[:, k : k + 1])
            for c in range(4):
                k = 4 * h + c
                if n < 9 and c >= 4 - 4:
                    nc.vector.tensor_scalar(
                        out=yg[:, c, :], in0=mx1[:, c, :], scalar1=gcol[:, k : k + 1], scalar2=gbcol[:, k : k + 1],
                        op0=ALU.mult, op1=ALU.add,
                    )
                else:
                    nc.scalar.activation(
                        out=yg[:, c, :], in_=mx1[:, c, :], func=ACT.Identity,
                        bias=gbcol[:, k : k + 1], scale=gcol[:, k : k + 1],
                    )
            yg_of[n], sq_of[n] = yg, sq

        def turn_y(n, bank):
            t1 = psum.tile([P, D], F32, name="t1", tag=bank, bufs=2 if bank == "mx1" else 1)
            for c in range(4):
                nc.tensor.transpose(t1[:, P * c : P * (c + 1)], yg_of[n][:, c, :], ident[:])
            t1_of[n] = t1

        def add_squares(n, misc):
            for c in range(4):
                nc.tensor.matmul(
                    misc[:, 0, :], lhsT=sq_of[n][:, c, :], rhs=ident[:], is_transpose=True,
                    start=(c == 0), stop=(c == 3),
                )

        def inverse_rms(n, misc):
            ss = work.tile([P, 1], F32, name="ss", tag="ss")
            junk = work.tile([P, P], F32, name="junk", tag="junk", bufs=2)
            nc.scalar.activation(out=junk[:], in_=misc[:, 0, :], func=ACT.Identity, accum_out=ss[:])
            rinv = work.tile([P, 1], F32, name="rinv", tag="rinv", bufs=4)
            nc.scalar.activation(out=rinv[:], in_=ss[:], func=ACT.Abs_reciprocal_sqrt, scale=1.0 / D)
            rinv_of[n] = rinv

        def rotate(n, on_vector):
            ww = work.tile([P, D // 2, 4], F32, name="ww", tag="ww")
            nc.vector.scalar_tensor_tensor(
                out=ww[:].rearrange("p r j -> p (r j)").rearrange("p (d k) -> p d k", k=2),
                in0=t1_of[n][:].unsqueeze(2).to_broadcast([P, D, 2]), scalar=rinv_of[n][:],
                in1=tab[:, n // H, :, :].rearrange("p r j -> p (r j)").rearrange("p (d k) -> p d k", k=2),
                op0=ALU.mult, op1=ALU.mult,
            )
            z = work.tile([P, D], BF16, name="z", tag="z", bufs=4, align_bytes=64)
            wv = ww[:].rearrange("i r j -> i (r j)").rearrange("i (p u s e) -> i s u p e", u=2, s=2, e=2)
            engine = nc.vector if on_vector else nc.gpsimd
            engine.tensor_tensor(
                out=z[:].rearrange("i (u p e) -> i u p e", u=2, e=2), in0=wv[:, 0], in1=wv[:, 1], op=ALU.add,
            )
            z_of[n] = z

        def turn_z(n, misc):
            words = z_of[n][:].bitcast(F32)
            for u in range(2):
                nc.tensor.transpose(misc[:, 1 + u, :], words[:, P * u : P * (u + 1)], ident[:])

        def leave_z(n, misc):
            q, k = divmod(n, 4)
            if k == 0:
                grp = work.tile([P, 4, P * 4], BF16, name="grp", tag="grp", bufs=2, align_bytes=64)
                grp_of[q] = grp
            nc.scalar.copy(
                out=grp_of[q][:, k, :].bitcast(F32).rearrange("p (i u) -> p i u", u=2),
                in_=misc[:, 1:3, :].rearrange("p u i -> p i u"),
            )

        def quantize(q):
            zc = work.tile([P, 512], U32, name="zc", tag="zc", bufs=2, align_bytes=64)
            zs = work.tile([P, 512], U8, name="zs", tag="zs", bufs=2, align_bytes=64)
            nc.vector.quantize_mx(out=zc[:].bitcast(FP8X4), scales=zs[:], in_=grp_of[q][:].rearrange("p n k -> p (n k)"))
            zc_of[q], zs_of[q] = zc, zs

        def second_matmul(q, st, extra):
            u_ps = psum.tile([P, 512], F32, name="u_ps", tag="mx1" if extra else "u", bufs=2)
            nc.tensor.matmul_mx(
                out=u_ps[:],
                lhsT=kc[:, 512 * st : 512 * (st + 1)].bitcast(FP8X4),
                lhsT_scale=ksc[:, P * st : P * (st + 1)],
                rhs=zc_of[q][:].bitcast(FP8X4),
                rhs_scale=zs_of[q][:],
                start=True,
                stop=True,
            )
            return u_ps

        def gate(q, st, u_ps, pair):
            a, b = divmod(q, NQ)
            gates = alpha_t[:, a, 4 * b : 4 * b + 4, :].rearrange("p h i -> p (h i)")
            v = work.tile([P, 512], F32, name="v", tag="v", bufs=10)
            nc.vector.scalar_tensor_tensor(
                out=v[:], in0=u_ps[:], scalar=nkb[:, st : st + 1], in1=gates, op0=ALU.max, op1=ALU.mult,
            )
            if pair:
                w = work.tile([P, 256], F32, name="w", tag="w", bufs=6)
                nc.gpsimd.tensor_tensor(out=w[:], in0=v[:, 0:256], in1=v[:, 256:512], op=ALU.add)
                return w, 2
            return v, 4

        count = {}

        def pool_heads(q, st, v, parts):
            a, b = divmod(q, NQ)
            half, sc = divmod(st, 4)
            done = count.get((a, half), 0)
            if done == 0:
                acc[half] = psum.tile([P, 512], F32, name=f"acc{half}", tag=f"acc{half}", bufs=1)
            last = done == 4 * NQ - 1
            for hh in range(parts):
                nc.tensor.matmul(
                    acc[half][:, P * sc : P * (sc + 1)], lhsT=v[:, P * hh : P * (hh + 1)], rhs=ident[:],
                    is_transpose=True,
                    start=(done == 0 and hh == 0),
                    stop=(last and hh == parts - 1),
                )
            count[(a, half)] = done + 1
            if last:
                o = work.tile([P, 512], F32, name="o", tag="o", bufs=2)
                nc.vector.scalar_tensor_tensor(
                    out=o[:], in0=kb_all[:, 512 * half : 512 * (half + 1)], scalar=asum4[:, a : a + 1],
                    in1=acc[half][:], op0=ALU.mult, op1=ALU.add,
                )
                nc.sync.dma_start(out=out[P * a : P * (a + 1), 512 * half : 512 * (half + 1)], in_=o[:])

        todo = [(q, st) for q in range(quads) for st in range(8)]
        rest = []
        ZL = 4
        WL = 2
        n = 0
        while n < units or todo or rest:
            steady = n < units
            if steady:
                mx1 = first_matmul(n)
            width = 2 if steady else 4
            items = []
            def scores():
                while todo and len(items) < width and todo[0][0] in zc_of and (not steady or n >= 4 * todo[0][0] + 5 + ZL):
                    q, st = todo.pop(0)
                    extra = len(items) >= 2
                    items.append((q, st, second_matmul(q, st, extra)))
            def gated():
                for q, st, u_ps in items:
                    pair = steady and (st % 2 == 0)
                    v, parts = gate(q, st, u_ps, pair)
                    rest.append((n + (WL if pair else 1), q, st, v, parts))
            def pooled():
                for item in [r for r in rest if r[0] <= n]:
                    rest.remove(item)
                    pool_heads(*item[1:])
            if steady:
                scores()
                if 0 <= n - 2:
                    rotate(n - 2, False)
                if n - ZL - 1 >= 0 and (n - ZL - 1) % 4 == 3:
                    quantize((n - ZL - 1) // 4)
                gated()
                leave_first(n, mx1)
                if n < 8:
                    a, b = divmod(n, NQ)
                    at_ps = spread_gates(a, b)
                if n >= 1:
                    misc = psum.tile([P, 4, P], F32, name="misc", tag="misc", bufs=1)
                    if n >= ZL:
                        turn_z(n - ZL, misc)
                    add_squares(n - 1, misc)
                pooled()
                if n >= 1:
                    turn_y(n - 1, ("t1", "acc0", "acc1")[n % 3] if n < 8 else "t1")
                    inverse_rms(n - 1, misc)
                if n >= ZL:
                    leave_z(n - ZL, misc)
                if n < 8:
                    nc.scalar.copy(out=alpha_t[:, a, 4 * b : 4 * b + 4, :], in_=at_ps[:])
                if n == 1:
                    x_scaled(1)
                if n == 3:
                    x_quantized(1, x_turned(1))
            elif n == units:
                scores()
                misc = psum.tile([P, 4, P], F32, name="misc", tag="mx1", bufs=2)
                add_squares(n - 1, misc)
                turn_z(n - ZL, misc)
                rotate(n - 2, False)
                quantize(quads - 2)
                gated()
                inverse_rms(n - 1, misc)
                leave_z(n - ZL, misc)
                turn_y(n - 1, "mx1")
                rotate(n - 1, True)
                pooled()
            elif n == units + 1:
                scores()
                misc = psum.tile([P, 4, P], F32, name="misc", tag="misc", bufs=1)
                late = psum.tile([P, 4, P], F32, name="late", tag="t1", bufs=1)
                turn_z(units - 3, misc)
                leave_z(units - 3, misc)
                turn_z(units - 2, late)
                leave_z(units - 2, late)
                pooled()
                last = psum.tile([P, 4, P], F32, name="last", tag="misc", bufs=1)
                turn_z(units - 1, last)
                leave_z(units - 1, last)
                gated()
                quantize(quads - 1)
            else:
                scores()
                gated()
                pooled()
            n += 1
